import numpy as np
import ml_dtypes


def mxq(x, axis, fmt="e4m3"):
    dtype, down = {"e4m3": (ml_dtypes.float8_e4m3fn, 7), "e5m2": (ml_dtypes.float8_e5m2, 14)}[fmt]
    v = np.moveaxis(np.asarray(x, np.float32).astype(ml_dtypes.bfloat16).astype(np.float64), axis, -1)
    blocks = v.reshape(v.shape[:-1] + (-1, 32))
    amax = np.abs(blocks).max(-1, keepdims=True)
    byte = np.maximum(np.where(amax > 0, np.frexp(amax)[1] - 1 + 127, 0) - down, 1)
    scale = np.exp2(byte - 127.0)
    codes = (blocks / scale).astype(np.float32).astype(dtype).astype(np.float64)
    return np.moveaxis((codes * scale).reshape(v.shape), -1, axis)


WIDE = False


def mx_kscale(k):
    if not WIDE:
        return np.ones(k)
    levels = np.array([18, -18])
    if k % 512:
        return np.exp2(np.random.permutation(np.resize(levels, k // 32))).repeat(32)
    a = np.empty((k // 512, 16))
    for p in range(k // 512):
        a[p, :8] = np.random.permutation(np.resize(levels, 8))
        for g in range(8):
            far = levels[np.abs(levels - a[p, g]) >= 10]
            a[p, g + 8] = far[np.random.randint(len(far))]
    return np.exp2(a.ravel()).repeat(32)


def f64(x):
    return np.asarray(x).astype(np.float64)


def striped(idx):
    return np.tile(np.asarray(idx).reshape(-1, 16).T, (8, 1)).astype(np.uint16)


def unstriped(offs):
    return offs[:16].T.reshape(-1).astype(np.int64)

def planes(y):
    n, m = y.shape
    v = y.astype(np.float32).astype(ml_dtypes.bfloat16).astype(np.float64).reshape(n // 32, 32, m)
    top = np.abs(v).max(1)
    byte = np.clip(np.where(top > 0, np.frexp(top)[1] - 1 + 127 - 7, 1), 1, 254)
    codes = (v * np.exp2(127.0 - byte)[:, None, :]).reshape(n, m).astype(np.float32).astype(ml_dtypes.float8_e4m3fn).view(np.uint8)
    words = codes.reshape(n // 512, 128, 4, m).transpose(0, 1, 3, 2)
    return np.ascontiguousarray(words), np.ascontiguousarray(byte.astype(np.uint8).reshape(n // 512, 16, m))


def setup_inputs():
    n = np.random.standard_normal
    uni = np.random.uniform
    idx = np.random.permutation(2048)[:512]
    f_e = mx_kscale(512)
    f_i = np.ones(2048)
    f_i[idx] = mx_kscale(512)
    return {
        "kT": (n((512, 2048)) / np.sqrt(512) * f_i[None, :]).astype(np.float32),
        "vT": (n((512, 2048)) / np.sqrt(512) / f_i[None, :]).astype(np.float32),
        "cd": (uni(0.75, 1.3, (512, 1))).astype(np.float32),
        "ce": np.tile(uni(0.75, 1.3, 512) * f_e, (128, 1)).astype(np.float32),
        "doT": (n((512, 512)) / f_e[:, None]).astype(np.float32),
        "offs": striped(idx),
    }


def reference(kT, vT, cd, ce, doT, offs):
    idx = unstriped(offs)
    kT_i = f64(kT)[:, idx]
    vT_i = f64(vT)[:, idx]
    S = mxq(kT_i, 1, "e4m3") @ mxq(vT_i, 1, "e4m3").T
    s = f64(cd) * f64(ce)[:1] * S
    out_0 = mxq(s, 1, "e4m3") @ mxq(f64(doT), 0, "e5m2")
    return (out_0,) + planes(out_0)

@@ -1,0 +1,170 @@
+from contextlib import ExitStack
+
+import concourse.mybir as mybir
+from concourse.masks import make_identity
+
+F32 = mybir.dt.float32
+BF16 = mybir.dt.bfloat16
+I32 = mybir.dt.int32
+U32 = mybir.dt.uint32
+U16 = mybir.dt.uint16
+U8 = mybir.dt.uint8
+E4M3 = mybir.dt.float8_e4m3fn_x4
+E5M2 = mybir.dt.float8_e5m2_x4
+MULT = mybir.AluOpType.mult
+
+P = 128
+PACK = 4
+D = 512
+T = 2048
+SLOTS = 512
+R = 512
+
+FLOPS = 2 * D * D * SLOTS + 2 * D * D * R
+BYTES = 4 * (2 * D * T + D + D + D * R + D * R) + 2 * P * SLOTS // 16 + D * R + D * R // 32
+
+
+def tile_attend_glin_q_pl_kernel(tc, kT, vT, cd, ce, doT, offs, out_0, out_1, out_2):
+    nc = tc.nc
+    with ExitStack() as ctx:
+        keep = ctx.enter_context(tc.tile_pool(name="keep", bufs=1))
+        turn_ps = ctx.enter_context(tc.psum_pool(name="turn_ps", bufs=2))
+        state_ps = ctx.enter_context(tc.psum_pool(name="state_ps", bufs=2))
+        out_ps = ctx.enter_context(tc.psum_pool(name="out_ps", bufs=4))
+
+        def sb(shape, dtype, name, tag=None):
+            return keep.tile(shape, dtype, name=name, tag=tag or name, align_bytes=64)
+
+        offsets = keep.tile([P, SLOTS // 16], U16, name="offsets")
+        v_pool = [sb([P, T], F32, "v_pool%d" % t) for t in range(PACK)]
+        k_pool = [sb([P, T], F32, "k_pool%d" % j) for j in range(PACK)]
+        do_raw = sb([P, PACK, R], F32, "do_raw")
+        cd_col = sb([P, PACK], F32, "cd_col")
+        ce_col = sb([P, PACK], F32, "ce_col")
+
+        v_rows = vT.rearrange("(m t) n -> m t n", t=PACK)
+        k_rows = kT.rearrange("(m j) n -> m j n", j=PACK)
+        nc.sync.dma_start(out=v_pool[0][:], in_=v_rows[:, 0, :])
+        nc.sync.dma_start(offsets[:], offs)
+        nc.scalar.dma_start(out=cd_col[:], in_=cd.rearrange("(m j) o -> m (j o)", j=PACK))
+        nc.scalar.dma_start(out=ce_col[:], in_=ce[0:1, :].rearrange("o (p t) -> (o p) t", t=PACK))
+        for t in range(1, PACK):
+            nc.sync.dma_start(out=v_pool[t][:], in_=v_rows[:, t, :])
+        nc.sync.dma_start(out=do_raw[:], in_=doT.rearrange("(p t) r -> p t r", t=PACK))
+        for j in range(PACK):
+            nc.sync.dma_start(out=k_pool[j][:], in_=k_rows[:, j, :])
+
+        ident = sb([P, P], F32, "ident")
+        make_identity(nc, ident[:])
+
+        cd_rows = state_ps.tile([P, PACK, P], F32, name="state")
+        for j in range(PACK):
+            nc.tensor.transpose(cd_rows[:, j, :], cd_col[:, j : j + 1].to_broadcast([P, P]), ident[:])
+        factor = [sb([P, P, PACK], F32, "factor%d" % j) for j in range(PACK)]
+        for j in range(PACK):
+            nc.vector.tensor_tensor(
+                factor[j][:],
+                cd_rows[:, j, :].unsqueeze(2).to_broadcast([P, P, PACK]),
+                ce_col[:].unsqueeze(1).to_broadcast([P, P, PACK]),
+                MULT,
+            )
+
+        def gather_and_turn(pool, name):
+            picked = sb([P, SLOTS], BF16, name + "_picked")
+            nc.vector.tensor_copy(picked[:], pool[:].indirect(offsets[:]))
+            pairs = picked[:].bitcast(F32)
+            turned = turn_ps.tile([P, 2, P], F32, name="turned")
+            for u in range(2):
+                nc.tensor.transpose(turned[:, u, :], pairs[:, u::2], ident[:])
+            grouped = sb([P, P * PACK], BF16, name + "_grouped")
+            nc.scalar.copy(
+                grouped[:].bitcast(F32).rearrange("p (m u) -> p m u", u=2),
+                turned[:].rearrange("p u m -> p m u"),
+            )
+            return grouped
+
+        def quantize(grouped, fmt, name, tag=None):
+            width = grouped.shape[1] // PACK
+            codes = sb([P, width], U32, name + "_codes", tag)
+            scales = sb([P, width], U8, name + "_scales")
+            nc.vector.quantize_mx(out=codes[:].bitcast(fmt), scales=scales[:], in_=grouped)
+            return codes, scales
+
+        def interleave(engine_copy, grouped, planes, lo, hi):
+            engine_copy(
+                grouped[:, lo * PACK : hi * PACK].rearrange("p (c i t) -> p c t i", i=4, t=PACK),
+                planes[:, :, lo:hi].rearrange("p t (c i) -> p c t i", i=4),
+            )
+
+        v_q = []
+        for t in range(PACK):
+            v_q.append(quantize(gather_and_turn(v_pool[t], "v%d" % t)[:], E4M3, "v%d" % t))
+
+        do_grouped = sb([P, R * PACK], BF16, "do_grouped")
+        for c in range(4):
+            interleave(nc.scalar.copy, do_grouped, do_raw, c * 128, (c + 1) * 128)
+        k_grouped = [gather_and_turn(k_pool[0], "k0")]
+        do_codes, do_scales = quantize(do_grouped[:], E5M2, "do", "k_pool0")
+
+        y = sb([P, PACK, R], F32, "y")
+        out_rows = out_0.rearrange("(m j) r -> m j r", j=PACK)
+        for j in range(PACK):
+            k_codes, k_scales = quantize(k_grouped[j][:], E4M3, "k%d" % j)
+            state = state_ps.tile([P, PACK, P], F32, name="state")
+            for t in range(PACK):
+                nc.tensor.matmul_mx(
+                    out=state[:, t, :],
+                    lhsT=v_q[t][0][:].bitcast(E4M3),
+                    lhsT_scale=v_q[t][1][:],
+                    rhs=k_codes[:].bitcast(E4M3),
+                    rhs_scale=k_scales[:],
+                    start=True,
+                    stop=True,
+                )
+            if j + 1 < PACK:
+                k_grouped.append(gather_and_turn(k_pool[j + 1], "k%d" % (j + 1)))
+            s_grouped = sb([P, P * PACK], BF16, "s%d_grouped" % j, "k_pool%d" % (j + 1))
+            nc.vector.tensor_tensor(
+                s_grouped[:].rearrange("p (m t) -> p m t", t=PACK),
+                state[:].rearrange("p t m -> p m t"),
+                factor[j][:],
+                MULT,
+            )
+            s_codes, s_scales = quantize(s_grouped[:], E4M3, "s%d" % j)
+            acc = out_ps.tile([P, R], F32, name="acc")
+            nc.tensor.matmul_mx(
+                out=acc[:],
+                lhsT=s_codes[:].bitcast(E4M3),
+                lhsT_scale=s_scales[:],
+                rhs=do_codes[:].bitcast(E5M2),
+                rhs_scale=do_scales[:],
+                start=True,
+                stop=True,
+            )
+            if j + 1 < PACK:
+                nc.scalar.copy(y[:, j, :], acc[:])
+            else:
+                nc.scalar.copy(y[:, j, 0:256], acc[:, 0:256])
+                nc.scalar.copy(y[:, j, 256:512], acc[:, 256:512])
+            nc.sync.dma_start(out=out_rows[:, j, :], in_=y[:, j, :])
+
+        y_grouped = sb([P, R * PACK], BF16, "y_grouped")
+        interleave(nc.vector.tensor_copy, y_grouped, y, 0, 256)
+        interleave(nc.vector.tensor_copy, y_grouped, y, 256, 384)
+        interleave(nc.scalar.copy, y_grouped, y, 384, 512)
+        y_codes = sb([P, R], U32, "y_codes")
+        y_scales = sb([P, R], U8, "y_scales")
+        words = out_1[0].rearrange("p c l -> p (c l)").bitcast(I32)
+        for lo in (0, 256):
+            nc.vector.quantize_mx(
+                out=y_codes[:, lo : lo + 256].bitcast(E4M3),
+                scales=y_scales[:, lo : lo + 256],
+                in_=y_grouped[:, lo * PACK : (lo + 256) * PACK],
+            )
+            nc.sync.dma_start(out=words[:, lo : lo + 256], in_=y_codes[:, lo : lo + 256].bitcast(I32))
+        for q in range(4):
+            queue = nc.sync if q == 3 else nc.scalar
+            queue.dma_start(
+                out=out_2[0, 4 * q : 4 * q + 4, :].bitcast(I32),
+                in_=y_scales[32 * q : 32 * q + 4, :].bitcast(I32),
+            )

@@ -28,16 +28,25 @@ def tile_attend_glin_q_pl_kernel(tc, kT, vT, cd, ce, doT, offs, out_0, out_1, ou
     nc = tc.nc
     with ExitStack() as ctx:
         keep = ctx.enter_context(tc.tile_pool(name="keep", bufs=1))
+        reused = ctx.enter_context(tc.tile_pool(name="reused", bufs=1))
         turn_ps = ctx.enter_context(tc.psum_pool(name="turn_ps", bufs=2))
-        state_ps = ctx.enter_context(tc.psum_pool(name="state_ps", bufs=2))
-        out_ps = ctx.enter_context(tc.psum_pool(name="out_ps", bufs=4))
+        state_ps = ctx.enter_context(tc.psum_pool(name="state_ps", bufs=3))
+        out_ps = ctx.enter_context(tc.psum_pool(name="out_ps", bufs=3))
 
-        def sb(shape, dtype, name, tag=None):
-            return keep.tile(shape, dtype, name=name, tag=tag or name, align_bytes=64)
+        def sb(shape, dtype, name, offset=None):
+            if offset is None:
+                return keep.tile(shape, dtype, name=name, align_bytes=64)
+            return reused.tile(shape, dtype, name=name, align_bytes=64, offset=offset)
+
+        def v_bytes(t):
+            return t * T * 4
+
+        def k_bytes(j):
+            return (PACK + j) * T * 4
 
         offsets = keep.tile([P, SLOTS // 16], U16, name="offsets")
-        v_pool = [sb([P, T], F32, "v_pool%d" % t) for t in range(PACK)]
-        k_pool = [sb([P, T], F32, "k_pool%d" % j) for j in range(PACK)]
+        v_pool = [sb([P, T], F32, "v_pool%d" % t, v_bytes(t)) for t in range(PACK)]
+        k_pool = [sb([P, T], F32, "k_pool%d" % j, k_bytes(j)) for j in range(PACK)]
         do_raw = sb([P, PACK, R], F32, "do_raw")
         cd_col = sb([P, PACK], F32, "cd_col")
         ce_col = sb([P, PACK], F32, "ce_col")
@@ -46,12 +55,13 @@ def tile_attend_glin_q_pl_kernel(tc, kT, vT, cd, ce, doT, offs, out_0, out_1, ou
         k_rows = kT.rearrange("(m j) n -> m j n", j=PACK)
         nc.sync.dma_start(out=v_pool[0][:], in_=v_rows[:, 0, :])
         nc.sync.dma_start(offsets[:], offs)
-        nc.scalar.dma_start(out=cd_col[:], in_=cd.rearrange("(m j) o -> m (j o)", j=PACK))
-        nc.scalar.dma_start(out=ce_col[:], in_=ce[0:1, :].rearrange("o (p t) -> (o p) t", t=PACK))
+        nc.sync.dma_start(out=cd_col[:], in_=cd.rearrange("(m j) o -> m (j o)", j=PACK))
+        nc.sync.dma_start(out=ce_col[:], in_=ce[0:1, :].rearrange("o (p t) -> (o p) t", t=PACK))
         for t in range(1, PACK):
             nc.sync.dma_start(out=v_pool[t][:], in_=v_rows[:, t, :])
-        nc.sync.dma_start(out=do_raw[:], in_=doT.rearrange("(p t) r -> p t r", t=PACK))
         for j in range(PACK):
+            if j == 2:
+                nc.sync.dma_start(out=do_raw[:], in_=doT.rearrange("(p t) r -> p t r", t=PACK))
             nc.sync.dma_start(out=k_pool[j][:], in_=k_rows[:, j, :])
 
         ident = sb([P, P], F32, "ident")
@@ -69,23 +79,23 @@ def tile_attend_glin_q_pl_kernel(tc, kT, vT, cd, ce, doT, offs, out_0, out_1, ou
                 MULT,
             )
 
-        def gather_and_turn(pool, name):
-            picked = sb([P, SLOTS], BF16, name + "_picked")
+        def gather_and_turn(pool, name, offset=None, picked_offset=None):
+            picked = sb([P, SLOTS], BF16, name + "_picked", picked_offset)
             nc.vector.tensor_copy(picked[:], pool[:].indirect(offsets[:]))
             pairs = picked[:].bitcast(F32)
             turned = turn_ps.tile([P, 2, P], F32, name="turned")
             for u in range(2):
                 nc.tensor.transpose(turned[:, u, :], pairs[:, u::2], ident[:])
-            grouped = sb([P, P * PACK], BF16, name + "_grouped")
+            grouped = sb([P, P * PACK], BF16, name + "_grouped", offset)
             nc.scalar.copy(
                 grouped[:].bitcast(F32).rearrange("p (m u) -> p m u", u=2),
                 turned[:].rearrange("p u m -> p m u"),
             )
             return grouped
 
-        def quantize(grouped, fmt, name, tag=None):
+        def quantize(grouped, fmt, name, offset=None):
             width = grouped.shape[1] // PACK
-            codes = sb([P, width], U32, name + "_codes", tag)
+            codes = sb([P, width], U32, name + "_codes", offset)
             scales = sb([P, width], U8, name + "_scales")
             nc.vector.quantize_mx(out=codes[:].bitcast(fmt), scales=scales[:], in_=grouped)
             return codes, scales
@@ -97,19 +107,19 @@ def tile_attend_glin_q_pl_kernel(tc, kT, vT, cd, ce, doT, offs, out_0, out_1, ou
             )
 
         v_q = []
+        v_grouped = [gather_and_turn(v_pool[0], "v0")]
         for t in range(PACK):
-            v_q.append(quantize(gather_and_turn(v_pool[t], "v%d" % t)[:], E4M3, "v%d" % t))
-
-        do_grouped = sb([P, R * PACK], BF16, "do_grouped")
-        for c in range(4):
-            interleave(nc.scalar.copy, do_grouped, do_raw, c * 128, (c + 1) * 128)
-        k_grouped = [gather_and_turn(k_pool[0], "k0")]
-        do_codes, do_scales = quantize(do_grouped[:], E5M2, "do", "k_pool0")
+            if t + 1 < PACK:
+                v_grouped.append(gather_and_turn(v_pool[t + 1], "v%d" % (t + 1)))
+            else:
+                k0 = gather_and_turn(k_pool[0], "k0")
+            v_q.append(quantize(v_grouped[t][:], E4M3, "v%d" % t, v_bytes(t + 1)))
 
         y = sb([P, PACK, R], F32, "y")
         out_rows = out_0.rearrange("(m j) r -> m j r", j=PACK)
-        for j in range(PACK):
-            k_codes, k_scales = quantize(k_grouped[j][:], E4M3, "k%d" % j)
+
+        def first_product(j, k_grouped, offset=None):
+            k_codes, k_scales = quantize(k_grouped[:], E4M3, "k%d" % j, offset)
             state = state_ps.tile([P, PACK, P], F32, name="state")
             for t in range(PACK):
                 nc.tensor.matmul_mx(
@@ -121,16 +131,19 @@ def tile_attend_glin_q_pl_kernel(tc, kT, vT, cd, ce, doT, offs, out_0, out_1, ou
                     start=True,
                     stop=True,
                 )
-            if j + 1 < PACK:
-                k_grouped.append(gather_and_turn(k_pool[j + 1], "k%d" % (j + 1)))
-            s_grouped = sb([P, P * PACK], BF16, "s%d_grouped" % j, "k_pool%d" % (j + 1))
+            return state
+
+        def weigh(j, state, offset=None):
+            s_grouped = sb([P, P * PACK], BF16, "s%d_grouped" % j, offset)
             nc.vector.tensor_tensor(
                 s_grouped[:].rearrange("p (m t) -> p m t", t=PACK),
                 state[:].rearrange("p t m -> p m t"),
                 factor[j][:],
                 MULT,
             )
-            s_codes, s_scales = quantize(s_grouped[:], E4M3, "s%d" % j)
+            return quantize(s_grouped[:], E4M3, "s%d" % j)
+
+        def second_product(j, s_codes, s_scales):
             acc = out_ps.tile([P, R], F32, name="acc")
             nc.tensor.matmul_mx(
                 out=acc[:],
@@ -147,6 +160,24 @@ def tile_attend_glin_q_pl_kernel(tc, kT, vT, cd, ce, doT, offs, out_0, out_1, ou
                 nc.scalar.copy(y[:, j, 0:256], acc[:, 0:256])
                 nc.scalar.copy(y[:, j, 256:512], acc[:, 256:512])
             nc.sync.dma_start(out=out_rows[:, j, :], in_=y[:, j, :])
+
+        k1 = gather_and_turn(k_pool[1], "k1", k_bytes(6), k_bytes(5))
+        do_grouped = sb([P, R * PACK], BF16, "do_grouped", k_bytes(5))
+        for c in range(4):
+            interleave(nc.scalar.copy, do_grouped, do_raw, c * 128, (c + 1) * 128)
+        state0 = first_product(0, k0, k_bytes(1))
+        state1 = first_product(1, k1)
+        s0 = weigh(0, state0, k_bytes(6))
+        s1 = weigh(1, state1)
+        k2 = gather_and_turn(k_pool[2], "k2")
+        do_codes, do_scales = quantize(do_grouped[:], E5M2, "do", k_bytes(2))
+        second_product(0, *s0)
+        second_product(1, *s1)
+        k3 = gather_and_turn(k_pool[3], "k3", k_bytes(4))
+        state2 = first_product(2, k2, k_bytes(3))
+        state3 = first_product(3, k3)
+        second_product(2, *weigh(2, state2, k_bytes(4)))
+        second_product(3, *weigh(3, state3))
 
         y_grouped = sb([P, R * PACK], BF16, "y_grouped")
         interleave(nc.vector.tensor_copy, y_grouped, y, 0, 256)

@@ -60,7 +60,7 @@ def tile_attend_glin_q_pl_kernel(tc, kT, vT, cd, ce, doT, offs, out_0, out_1, ou
         for t in range(1, PACK):
             nc.sync.dma_start(out=v_pool[t][:], in_=v_rows[:, t, :])
         for j in range(PACK):
-            if j == 2:
+            if j == 3:
                 nc.sync.dma_start(out=do_raw[:], in_=doT.rearrange("(p t) r -> p t r", t=PACK))
             nc.sync.dma_start(out=k_pool[j][:], in_=k_rows[:, j, :])
 
@@ -133,17 +133,31 @@ def tile_attend_glin_q_pl_kernel(tc, kT, vT, cd, ce, doT, offs, out_0, out_1, ou
                 )
             return state
 
-        def weigh(j, state, offset=None):
+        def weigh(j, state, offset=None, parts=1):
             s_grouped = sb([P, P * PACK], BF16, "s%d_grouped" % j, offset)
-            nc.vector.tensor_tensor(
-                s_grouped[:].rearrange("p (m t) -> p m t", t=PACK),
-                state[:].rearrange("p t m -> p m t"),
-                factor[j][:],
-                MULT,
-            )
-            return quantize(s_grouped[:], E4M3, "s%d" % j)
+            width = P // parts
+            for lo in range(0, P, width):
+                nc.vector.tensor_tensor(
+                    s_grouped[:, lo * PACK : (lo + width) * PACK].rearrange("p (m t) -> p m t", t=PACK),
+                    state[:, :, lo : lo + width].rearrange("p t m -> p m t"),
+                    factor[j][:, lo : lo + width, :],
+                    MULT,
+                )
+            return s_grouped
 
-        def second_product(j, s_codes, s_scales):
+        def second_product(j, s_grouped, offset=None, parts=1):
+            s_codes = sb([P, P], U32, "s%d_codes" % j, offset)
+            s_scales = sb([P, P], U8, "s%d_scales" % j)
+            width = P // parts
+            for lo in range(0, P, width):
+                nc.vector.quantize_mx(
+                    out=s_codes[:, lo : lo + width].bitcast(E4M3),
+                    scales=s_scales[:, lo : lo + width],
+                    in_=s_grouped[:, lo * PACK : (lo + width) * PACK],
+                )
+            return s_codes, s_scales
+
+        def multiply(s_codes, s_scales):
             acc = out_ps.tile([P, R], F32, name="acc")
             nc.tensor.matmul_mx(
                 out=acc[:],
@@ -154,35 +168,48 @@ def tile_attend_glin_q_pl_kernel(tc, kT, vT, cd, ce, doT, offs, out_0, out_1, ou
                 start=True,
                 stop=True,
             )
-            if j + 1 < PACK:
-                nc.scalar.copy(y[:, j, :], acc[:])
-            else:
-                nc.scalar.copy(y[:, j, 0:256], acc[:, 0:256])
-                nc.scalar.copy(y[:, j, 256:512], acc[:, 256:512])
+            return acc
+
+        def hand_out(j, acc):
+            nc.scalar.copy(y[:, j, :], acc[:])
             nc.sync.dma_start(out=out_rows[:, j, :], in_=y[:, j, :])
 
-        k1 = gather_and_turn(k_pool[1], "k1", k_bytes(6), k_bytes(5))
+        k1 = gather_and_turn(k_pool[1], "k1")
+        state0 = first_product(0, k0, k_bytes(1))
+        k2 = gather_and_turn(k_pool[2], "k2", k_bytes(6), k_bytes(5))
         do_grouped = sb([P, R * PACK], BF16, "do_grouped", k_bytes(5))
         for c in range(4):
             interleave(nc.scalar.copy, do_grouped, do_raw, c * 128, (c + 1) * 128)
-        state0 = first_product(0, k0, k_bytes(1))
-        state1 = first_product(1, k1)
-        s0 = weigh(0, state0, k_bytes(6))
-        s1 = weigh(1, state1)
-        k2 = gather_and_turn(k_pool[2], "k2")
-        do_codes, do_scales = quantize(do_grouped[:], E5M2, "do", k_bytes(2))
-        second_product(0, *s0)
-        second_product(1, *s1)
+        state1 = first_product(1, k1, k_bytes(2))
+        s0 = second_product(0, weigh(0, state0, k_bytes(2) + 1024))
+        state2 = first_product(2, k2)
+        s1 = weigh(1, state1, k_bytes(6))
         k3 = gather_and_turn(k_pool[3], "k3", k_bytes(4))
-        state2 = first_product(2, k2, k_bytes(3))
+        do_codes, do_scales = quantize(do_grouped[:], E5M2, "do", k_bytes(3))
+        s2 = weigh(2, state2, k_bytes(3) + 4096)
+        hand_out(0, multiply(*s0))
         state3 = first_product(3, k3)
-        second_product(2, *weigh(2, state2, k_bytes(4)))
-        second_product(3, *weigh(3, state3))
+        hand_out(1, multiply(*second_product(1, s1, k_bytes(4))))
+        hand_out(2, multiply(*second_product(2, s2, k_bytes(4) + 512)))
+        acc = multiply(*second_product(3, weigh(3, state3, None, 2), None, 2))
 
         y_grouped = sb([P, R * PACK], BF16, "y_grouped")
-        interleave(nc.vector.tensor_copy, y_grouped, y, 0, 256)
-        interleave(nc.vector.tensor_copy, y_grouped, y, 256, 384)
-        interleave(nc.scalar.copy, y_grouped, y, 384, 512)
+        y_places = y_grouped[:].rearrange("p (r j) -> p r j", j=PACK)
+
+        def first_places(engine_copy, lo, hi):
+            engine_copy(
+                y_places[:, lo:hi, 0:3].rearrange("p (c i) t -> p c t i", i=4),
+                y[:, 0:3, lo:hi].rearrange("p t (c i) -> p c t i", i=4),
+            )
+
+        first_places(nc.vector.tensor_copy, 0, 384)
+        first_places(nc.scalar.copy, 384, 512)
+        for lo in range(0, 384, 128):
+            nc.scalar.copy(y[:, 3, lo : lo + 128], acc[:, lo : lo + 128])
+            nc.vector.tensor_copy(y_places[:, lo : lo + 128, 3], y[:, 3, lo : lo + 128])
+        nc.scalar.copy(y_places[:, 384:512, 3], acc[:, 384:512])
+        nc.scalar.copy(y[:, 3, 384:512], acc[:, 384:512])
+        nc.sync.dma_start(out=out_rows[:, 3, :], in_=y[:, 3, :])
         y_codes = sb([P, R], U32, "y_codes")
         y_scales = sb([P, R], U8, "y_scales")
         words = out_1[0].rearrange("p c l -> p (c l)").bitcast(I32)

@@ -118,8 +118,7 @@ def tile_attend_glin_q_pl_kernel(tc, kT, vT, cd, ce, doT, offs, out_0, out_1, ou
         y = sb([P, PACK, R], F32, "y")
         out_rows = out_0.rearrange("(m j) r -> m j r", j=PACK)
 
-        def first_product(j, k_grouped, offset=None):
-            k_codes, k_scales = quantize(k_grouped[:], E4M3, "k%d" % j, offset)
+        def first_product(k_codes, k_scales):
             state = state_ps.tile([P, PACK, P], F32, name="state")
             for t in range(PACK):
                 nc.tensor.matmul_mx(
@@ -157,8 +156,7 @@ def tile_attend_glin_q_pl_kernel(tc, kT, vT, cd, ce, doT, offs, out_0, out_1, ou
                 )
             return s_codes, s_scales
 
-        def multiply(s_codes, s_scales):
-            acc = out_ps.tile([P, R], F32, name="acc")
+        def multiply(acc, s_codes, s_scales):
             nc.tensor.matmul_mx(
                 out=acc[:],
                 lhsT=s_codes[:].bitcast(E4M3),
@@ -170,45 +168,46 @@ def tile_attend_glin_q_pl_kernel(tc, kT, vT, cd, ce, doT, offs, out_0, out_1, ou
             )
             return acc
 
-        def hand_out(j, acc):
+        def hand_out(j, s_q):
+            acc = multiply(out_ps.tile([P, R], F32, name="acc"), *s_q)
             nc.scalar.copy(y[:, j, :], acc[:])
             nc.sync.dma_start(out=out_rows[:, j, :], in_=y[:, j, :])
 
         k1 = gather_and_turn(k_pool[1], "k1")
-        state0 = first_product(0, k0, k_bytes(1))
-        k2 = gather_and_turn(k_pool[2], "k2", k_bytes(6), k_bytes(5))
+        state0 = first_product(*quantize(k0[:], E4M3, "k0", k_bytes(1)))
+        k2 = gather_and_turn(k_pool[2], "k2", None, k_bytes(5))
         do_grouped = sb([P, R * PACK], BF16, "do_grouped", k_bytes(5))
         for c in range(4):
             interleave(nc.scalar.copy, do_grouped, do_raw, c * 128, (c + 1) * 128)
-        state1 = first_product(1, k1, k_bytes(2))
+        state1 = first_product(*quantize(k1[:], E4M3, "k1", k_bytes(2)))
         s0 = second_product(0, weigh(0, state0, k_bytes(2) + 1024))
-        state2 = first_product(2, k2)
-        s1 = weigh(1, state1, k_bytes(6))
+        s1 = weigh(1, state1)
+        k2_q = quantize(k2[:], E4M3, "k2")
+        state2 = first_product(*k2_q)
+        first_product(*k2_q)
+        first_product(*k2_q)
         k3 = gather_and_turn(k_pool[3], "k3", k_bytes(4))
         do_codes, do_scales = quantize(do_grouped[:], E5M2, "do", k_bytes(3))
-        s2 = weigh(2, state2, k_bytes(3) + 4096)
-        hand_out(0, multiply(*s0))
-        state3 = first_product(3, k3)
-        hand_out(1, multiply(*second_product(1, s1, k_bytes(4))))
-        hand_out(2, multiply(*second_product(2, s2, k_bytes(4) + 512)))
-        acc = multiply(*second_product(3, weigh(3, state3, None, 2), None, 2))
+        s2 = weigh(2, state2, k_bytes(3) + 2048)
+        hand_out(0, s0)
+        state3 = first_product(*quantize(k3[:], E4M3, "k3"))
+        hand_out(1, second_product(1, s1, k_bytes(4)))
+        hand_out(2, second_product(2, s2, k_bytes(4) + 512))
+        acc = multiply(out_ps.tile([P, R], F32, name="acc"), *second_product(3, weigh(3, state3, None, 2), None, 2))
 
         y_grouped = sb([P, R * PACK], BF16, "y_grouped")
         y_places = y_grouped[:].rearrange("p (r j) -> p r j", j=PACK)
 
-        def first_places(engine_copy, lo, hi):
+        def pair_of_places(engine_copy, first, lo, hi):
             engine_copy(
-                y_places[:, lo:hi, 0:3].rearrange("p (c i) t -> p c t i", i=4),
-                y[:, 0:3, lo:hi].rearrange("p t (c i) -> p c t i", i=4),
+                y_places[:, lo:hi, first : first + 2].rearrange("p (c i) t -> p c t i", i=4),
+                y[:, first : first + 2, lo:hi].rearrange("p t (c i) -> p c t i", i=4),
             )
 
-        first_places(nc.vector.tensor_copy, 0, 384)
-        first_places(nc.scalar.copy, 384, 512)
-        for lo in range(0, 384, 128):
+        pair_of_places(nc.vector.tensor_copy, 0, 0, R)
+        for lo in range(0, R, 128):
             nc.scalar.copy(y[:, 3, lo : lo + 128], acc[:, lo : lo + 128])
-            nc.vector.tensor_copy(y_places[:, lo : lo + 128, 3], y[:, 3, lo : lo + 128])
-        nc.scalar.copy(y_places[:, 384:512, 3], acc[:, 384:512])
-        nc.scalar.copy(y[:, 3, 384:512], acc[:, 384:512])
+            pair_of_places(nc.scalar.copy if lo == 384 else nc.vector.tensor_copy, 2, lo, lo + 128)
         nc.sync.dma_start(out=out_rows[:, 3, :], in_=y[:, 3, :])
         y_codes = sb([P, R], U32, "y_codes")
         y_scales = sb([P, R], U8, "y_scales")

@@ -19,6 +19,7 @@ D = 512
 T = 2048
 SLOTS = 512
 R = 512
+HALF = P // 2
 
 FLOPS = 2 * D * D * SLOTS + 2 * D * D * R
 BYTES = 4 * (2 * D * T + D + D + D * R + D * R) + 2 * P * SLOTS // 16 + D * R + D * R // 32
@@ -38,35 +39,38 @@ def tile_attend_glin_q_pl_kernel(tc, kT, vT, cd, ce, doT, offs, out_0, out_1, ou
                 return keep.tile(shape, dtype, name=name, align_bytes=64)
             return reused.tile(shape, dtype, name=name, align_bytes=64, offset=offset)
 
-        def v_bytes(t):
-            return t * T * 4
-
         def k_bytes(j):
-            return (PACK + j) * T * 4
+            return j * T * 4
 
         offsets = keep.tile([P, SLOTS // 16], U16, name="offsets")
-        v_pool = [sb([P, T], F32, "v_pool%d" % t, v_bytes(t)) for t in range(PACK)]
+        v_pool = [sb([P, T], F32, "v_pool%d" % t) for t in range(PACK)]
         k_pool = [sb([P, T], F32, "k_pool%d" % j, k_bytes(j)) for j in range(PACK)]
         do_raw = sb([P, PACK, R], F32, "do_raw")
-        cd_col = sb([P, PACK], F32, "cd_col")
-        ce_col = sb([P, PACK], F32, "ce_col")
+        rows = sb([P, D], F32, "rows")
+        nc.vector.memset(rows[:], 0.0)
 
         v_rows = vT.rearrange("(m t) n -> m t n", t=PACK)
         k_rows = kT.rearrange("(m j) n -> m j n", j=PACK)
         nc.sync.dma_start(out=v_pool[0][:], in_=v_rows[:, 0, :])
         nc.sync.dma_start(offsets[:], offs)
-        nc.sync.dma_start(out=cd_col[:], in_=cd.rearrange("(m j) o -> m (j o)", j=PACK))
-        nc.sync.dma_start(out=ce_col[:], in_=ce[0:1, :].rearrange("o (p t) -> (o p) t", t=PACK))
+        nc.sync.dma_start(out=rows[0:1, :], in_=cd.rearrange("d o -> o d"))
+        nc.sync.dma_start(out=rows[1:2, :], in_=ce[0:1, :])
         for t in range(1, PACK):
             nc.sync.dma_start(out=v_pool[t][:], in_=v_rows[:, t, :])
         for j in range(PACK):
-            if j == 3:
+            if j == PACK - 1:
                 nc.sync.dma_start(out=do_raw[:], in_=doT.rearrange("(p t) r -> p t r", t=PACK))
             nc.sync.dma_start(out=k_pool[j][:], in_=k_rows[:, j, :])
 
         ident = sb([P, P], F32, "ident")
         make_identity(nc, ident[:])
 
+        columns_ps = state_ps.tile([P, PACK, P], F32, name="state")
+        for j in range(PACK):
+            nc.tensor.transpose(columns_ps[:, j, :], rows[:, j::PACK], ident[:])
+        columns = sb([P, 2, PACK], F32, "columns")
+        nc.scalar.copy(columns[:], columns_ps[:, :, 0:2].rearrange("p j w -> p w j"))
+        cd_col, ce_col = columns[:, 0, :], columns[:, 1, :]
         cd_rows = state_ps.tile([P, PACK, P], F32, name="state")
         for j in range(PACK):
             nc.tensor.transpose(cd_rows[:, j, :], cd_col[:, j : j + 1].to_broadcast([P, P]), ident[:])
@@ -75,23 +79,27 @@ def tile_attend_glin_q_pl_kernel(tc, kT, vT, cd, ce, doT, offs, out_0, out_1, ou
             nc.vector.tensor_tensor(
                 factor[j][:],
                 cd_rows[:, j, :].unsqueeze(2).to_broadcast([P, P, PACK]),
-                ce_col[:].unsqueeze(1).to_broadcast([P, P, PACK]),
+                ce_col.unsqueeze(1).to_broadcast([P, P, PACK]),
                 MULT,
             )
 
-        def gather_and_turn(pool, name, offset=None, picked_offset=None):
-            picked = sb([P, SLOTS], BF16, name + "_picked", picked_offset)
+        picks = {}
+
+        def gather_and_turn(pool, name, offset=None):
+            picked = sb([P, SLOTS], BF16, name + "_picked", offset)
+            picks[name] = picked
             nc.vector.tensor_copy(picked[:], pool[:].indirect(offsets[:]))
             pairs = picked[:].bitcast(F32)
             turned = turn_ps.tile([P, 2, P], F32, name="turned")
             for u in range(2):
                 nc.tensor.transpose(turned[:, u, :], pairs[:, u::2], ident[:])
-            grouped = sb([P, P * PACK], BF16, name + "_grouped", offset)
+            return turned
+
+        def group(grouped, turned, lo=0, hi=P):
             nc.scalar.copy(
-                grouped[:].bitcast(F32).rearrange("p (m u) -> p m u", u=2),
-                turned[:].rearrange("p u m -> p m u"),
+                grouped[:, lo * PACK : hi * PACK].bitcast(F32).rearrange("p (m u) -> p m u", u=2),
+                turned[:, :, lo:hi].rearrange("p u m -> p m u"),
             )
-            return grouped
 
         def quantize(grouped, fmt, name, offset=None):
             width = grouped.shape[1] // PACK
@@ -106,57 +114,35 @@ def tile_attend_glin_q_pl_kernel(tc, kT, vT, cd, ce, doT, offs, out_0, out_1, ou
                 planes[:, :, lo:hi].rearrange("p t (c i) -> p c t i", i=4),
             )
 
-        v_q = []
-        v_grouped = [gather_and_turn(v_pool[0], "v0")]
-        for t in range(PACK):
-            if t + 1 < PACK:
-                v_grouped.append(gather_and_turn(v_pool[t + 1], "v%d" % (t + 1)))
-            else:
-                k0 = gather_and_turn(k_pool[0], "k0")
-            v_q.append(quantize(v_grouped[t][:], E4M3, "v%d" % t, v_bytes(t + 1)))
-
-        y = sb([P, PACK, R], F32, "y")
-        out_rows = out_0.rearrange("(m j) r -> m j r", j=PACK)
-
-        def first_product(k_codes, k_scales):
-            state = state_ps.tile([P, PACK, P], F32, name="state")
+        def first_product(k_codes, k_scales, lo=0, hi=P):
+            state = state_ps.tile([P, PACK, hi - lo], F32, name="state")
             for t in range(PACK):
                 nc.tensor.matmul_mx(
                     out=state[:, t, :],
-                    lhsT=v_q[t][0][:].bitcast(E4M3),
-                    lhsT_scale=v_q[t][1][:],
-                    rhs=k_codes[:].bitcast(E4M3),
-                    rhs_scale=k_scales[:],
+                    lhsT=v_codes[:, t * P : (t + 1) * P].bitcast(E4M3),
+                    lhsT_scale=v_scales[:, t * P : (t + 1) * P],
+                    rhs=k_codes[:, lo:hi].bitcast(E4M3),
+                    rhs_scale=k_scales[:, lo:hi],
                     start=True,
                     stop=True,
                 )
             return state
 
-        def weigh(j, state, offset=None, parts=1):
+        def weigh_columns(s_grouped, j, state, lo, hi):
+            nc.vector.tensor_tensor(
+                s_grouped[:, lo * PACK : hi * PACK].rearrange("p (m t) -> p m t", t=PACK),
+                state.rearrange("p t m -> p m t"),
+                factor[j][:, lo:hi, :],
+                MULT,
+            )
+
+        def weigh(j, state, offset=None):
             s_grouped = sb([P, P * PACK], BF16, "s%d_grouped" % j, offset)
-            width = P // parts
-            for lo in range(0, P, width):
-                nc.vector.tensor_tensor(
-                    s_grouped[:, lo * PACK : (lo + width) * PACK].rearrange("p (m t) -> p m t", t=PACK),
-                    state[:, :, lo : lo + width].rearrange("p t m -> p m t"),
-                    factor[j][:, lo : lo + width, :],
-                    MULT,
-                )
+            weigh_columns(s_grouped, j, state[:], 0, P)
             return s_grouped
 
-        def second_product(j, s_grouped, offset=None, parts=1):
-            s_codes = sb([P, P], U32, "s%d_codes" % j, offset)
-            s_scales = sb([P, P], U8, "s%d_scales" % j)
-            width = P // parts
-            for lo in range(0, P, width):
-                nc.vector.quantize_mx(
-                    out=s_codes[:, lo : lo + width].bitcast(E4M3),
-                    scales=s_scales[:, lo : lo + width],
-                    in_=s_grouped[:, lo * PACK : (lo + width) * PACK],
-                )
-            return s_codes, s_scales
-
-        def multiply(acc, s_codes, s_scales):
+        def multiply(s_codes, s_scales):
+            acc = out_ps.tile([P, R], F32, name="acc")
             nc.tensor.matmul_mx(
                 out=acc[:],
                 lhsT=s_codes[:].bitcast(E4M3),
@@ -168,32 +154,72 @@ def tile_attend_glin_q_pl_kernel(tc, kT, vT, cd, ce, doT, offs, out_0, out_1, ou
             )
             return acc
 
-        def hand_out(j, s_q):
-            acc = multiply(out_ps.tile([P, R], F32, name="acc"), *s_q)
+        def quantize_columns(codes, scales, grouped, fmt, lo, hi):
+            nc.vector.quantize_mx(
+                out=codes[:, lo:hi].bitcast(fmt),
+                scales=scales[:, lo:hi],
+                in_=grouped[:, lo * PACK : hi * PACK],
+            )
+
+        v_grouped = sb([P, D * PACK], BF16, "v_grouped")
+        for t in range(PACK):
+            group(v_grouped[:, t * P * PACK : (t + 1) * P * PACK], gather_and_turn(v_pool[t], "v%d" % t))
+
+        out_rows = out_0.rearrange("(m j) r -> m j r", j=PACK)
+
+        def hand_out(j, acc):
             nc.scalar.copy(y[:, j, :], acc[:])
             nc.sync.dma_start(out=out_rows[:, j, :], in_=y[:, j, :])
 
-        k1 = gather_and_turn(k_pool[1], "k1")
+        k0 = sb([P, P * PACK], BF16, "k0_grouped")
+        group(k0, gather_and_turn(k_pool[0], "k0"))
+        v_codes, v_scales = quantize(v_grouped[:], E4M3, "v", k_bytes(0))
+        k1 = sb([P, P * PACK], BF16, "k1_grouped")
+        group(k1, gather_and_turn(k_pool[1], "k1"))
         state0 = first_product(*quantize(k0[:], E4M3, "k0", k_bytes(1)))
-        k2 = gather_and_turn(k_pool[2], "k2", None, k_bytes(5))
-        do_grouped = sb([P, R * PACK], BF16, "do_grouped", k_bytes(5))
-        for c in range(4):
-            interleave(nc.scalar.copy, do_grouped, do_raw, c * 128, (c + 1) * 128)
+        k2 = sb([P, P * PACK], BF16, "k2_grouped", k_bytes(PACK + 2))
+        group(k2, gather_and_turn(k_pool[2], "k2", k_bytes(PACK + 1)))
+        do_grouped = sb([P, R * PACK], BF16, "do_grouped", k_bytes(PACK + 1))
+        for lo in range(0, R, 128):
+            interleave(nc.scalar.copy, do_grouped, do_raw, lo, lo + 128)
         state1 = first_product(*quantize(k1[:], E4M3, "k1", k_bytes(2)))
-        s0 = second_product(0, weigh(0, state0, k_bytes(2) + 1024))
-        s1 = weigh(1, state1)
+        s0 = quantize(weigh(0, state0, k_bytes(2) + 1024)[:], E4M3, "s0")
         k2_q = quantize(k2[:], E4M3, "k2")
+        s1_grouped = weigh(1, state1, k_bytes(PACK + 2))
         state2 = first_product(*k2_q)
-        first_product(*k2_q)
-        first_product(*k2_q)
-        k3 = gather_and_turn(k_pool[3], "k3", k_bytes(4))
+        warm = out_ps.tile([P, R], F32, name="acc")
+        for w in range(2):
+            nc.tensor.matmul_mx(
+                out=warm[:],
+                lhsT=k2_q[0][:].bitcast(E4M3),
+                lhsT_scale=k2_q[1][:],
+                rhs=v_codes[:].bitcast(E4M3),
+                rhs_scale=v_scales[:],
+                start=True,
+                stop=True,
+            )
+        turned3 = gather_and_turn(k_pool[3], "k3")
         do_codes, do_scales = quantize(do_grouped[:], E5M2, "do", k_bytes(3))
-        s2 = weigh(2, state2, k_bytes(3) + 2048)
-        hand_out(0, s0)
-        state3 = first_product(*quantize(k3[:], E4M3, "k3"))
-        hand_out(1, second_product(1, s1, k_bytes(4)))
-        hand_out(2, second_product(2, s2, k_bytes(4) + 512))
-        acc = multiply(out_ps.tile([P, R], F32, name="acc"), *second_product(3, weigh(3, state3, None, 2), None, 2))
+        s1 = quantize(s1_grouped[:], E4M3, "s1", k_bytes(3) + 4096)
+        s2_grouped = weigh(2, state2, k_bytes(3) + 2048)
+        acc0 = multiply(*s0)
+        acc1 = multiply(*s1)
+        k3 = sb([P, P * PACK], BF16, "k3_grouped", k_bytes(PACK))
+        group(k3, turned3)
+        whole3 = first_product(*quantize(k3[:], E4M3, "k3"))
+        state3 = [whole3[:, :, lo : lo + HALF] for lo in (0, HALF)]
+        y = sb([P, PACK, R], F32, "y", k_bytes(PACK) + 512)
+        hand_out(0, acc0)
+        hand_out(1, acc1)
+        hand_out(2, multiply(*quantize(s2_grouped[:], E4M3, "s2", k_bytes(PACK))))
+        s3_grouped = sb([P, P * PACK], BF16, "s3_grouped")
+        s3_codes = sb([P, P], U32, "s3_codes")
+        s3_scales = sb([P, P], U8, "s3_scales")
+        for h in range(2):
+            weigh_columns(s3_grouped, 3, state3[h], h * HALF, (h + 1) * HALF)
+        for lo in (0, HALF):
+            quantize_columns(s3_codes, s3_scales, s3_grouped, E4M3, lo, lo + HALF)
+        acc = multiply(s3_codes, s3_scales)
 
         y_grouped = sb([P, R * PACK], BF16, "y_grouped")
         y_places = y_grouped[:].rearrange("p (r j) -> p r j", j=PACK)
@@ -213,11 +239,7 @@ def tile_attend_glin_q_pl_kernel(tc, kT, vT, cd, ce, doT, offs, out_0, out_1, ou
         y_scales = sb([P, R], U8, "y_scales")
         words = out_1[0].rearrange("p c l -> p (c l)").bitcast(I32)
         for lo in (0, 256):
-            nc.vector.quantize_mx(
-                out=y_codes[:, lo : lo + 256].bitcast(E4M3),
-                scales=y_scales[:, lo : lo + 256],
-                in_=y_grouped[:, lo * PACK : (lo + 256) * PACK],
-            )
+            quantize_columns(y_codes, y_scales, y_grouped, E4M3, lo, lo + 256)
             nc.sync.dma_start(out=words[:, lo : lo + 256], in_=y_codes[:, lo : lo + 256].bitcast(I32))
         for q in range(4):
             queue = nc.sync if q == 3 else nc.scalar

@@ -165,6 +165,7 @@ def tile_attend_glin_q_pl_kernel(tc, kT, vT, cd, ce, doT, offs, out_0, out_1, ou
         for t in range(PACK):
             group(v_grouped[:, t * P * PACK : (t + 1) * P * PACK], gather_and_turn(v_pool[t], "v%d" % t))
 
+        y = sb([P, PACK, R], F32, "y")
         out_rows = out_0.rearrange("(m j) r -> m j r", j=PACK)
 
         def hand_out(j, acc):
@@ -177,15 +178,15 @@ def tile_attend_glin_q_pl_kernel(tc, kT, vT, cd, ce, doT, offs, out_0, out_1, ou
         k1 = sb([P, P * PACK], BF16, "k1_grouped")
         group(k1, gather_and_turn(k_pool[1], "k1"))
         state0 = first_product(*quantize(k0[:], E4M3, "k0", k_bytes(1)))
-        k2 = sb([P, P * PACK], BF16, "k2_grouped", k_bytes(PACK + 2))
+        k2 = sb([P, P * PACK], BF16, "k2_grouped")
         group(k2, gather_and_turn(k_pool[2], "k2", k_bytes(PACK + 1)))
         do_grouped = sb([P, R * PACK], BF16, "do_grouped", k_bytes(PACK + 1))
         for lo in range(0, R, 128):
             interleave(nc.scalar.copy, do_grouped, do_raw, lo, lo + 128)
         state1 = first_product(*quantize(k1[:], E4M3, "k1", k_bytes(2)))
         s0 = quantize(weigh(0, state0, k_bytes(2) + 1024)[:], E4M3, "s0")
+        s1_grouped = weigh(1, state1)
         k2_q = quantize(k2[:], E4M3, "k2")
-        s1_grouped = weigh(1, state1, k_bytes(PACK + 2))
         state2 = first_product(*k2_q)
         warm = out_ps.tile([P, R], F32, name="acc")
         for w in range(2):
@@ -200,18 +201,14 @@ def tile_attend_glin_q_pl_kernel(tc, kT, vT, cd, ce, doT, offs, out_0, out_1, ou
             )
         turned3 = gather_and_turn(k_pool[3], "k3")
         do_codes, do_scales = quantize(do_grouped[:], E5M2, "do", k_bytes(3))
-        s1 = quantize(s1_grouped[:], E4M3, "s1", k_bytes(3) + 4096)
         s2_grouped = weigh(2, state2, k_bytes(3) + 2048)
-        acc0 = multiply(*s0)
-        acc1 = multiply(*s1)
         k3 = sb([P, P * PACK], BF16, "k3_grouped", k_bytes(PACK))
         group(k3, turned3)
+        hand_out(0, multiply(*s0))
         whole3 = first_product(*quantize(k3[:], E4M3, "k3"))
         state3 = [whole3[:, :, lo : lo + HALF] for lo in (0, HALF)]
-        y = sb([P, PACK, R], F32, "y", k_bytes(PACK) + 512)
-        hand_out(0, acc0)
-        hand_out(1, acc1)
-        hand_out(2, multiply(*quantize(s2_grouped[:], E4M3, "s2", k_bytes(PACK))))
+        hand_out(1, multiply(*quantize(s1_grouped[:], E4M3, "s1", k_bytes(PACK))))
+        hand_out(2, multiply(*quantize(s2_grouped[:], E4M3, "s2", k_bytes(PACK) + 512)))
         s3_grouped = sb([P, P * PACK], BF16, "s3_grouped")
         s3_codes = sb([P, P], U32, "s3_codes")
         s3_scales = sb([P, P], U8, "s3_scales")

@@ -20,6 +20,7 @@ T = 2048
 SLOTS = 512
 R = 512
 HALF = P // 2
+SCALAR_COLUMNS = 352
 
 FLOPS = 2 * D * D * SLOTS + 2 * D * D * R
 BYTES = 4 * (2 * D * T + D + D + D * R + D * R) + 2 * P * SLOTS // 16 + D * R + D * R // 32
@@ -31,8 +32,8 @@ def tile_attend_glin_q_pl_kernel(tc, kT, vT, cd, ce, doT, offs, out_0, out_1, ou
         keep = ctx.enter_context(tc.tile_pool(name="keep", bufs=1))
         reused = ctx.enter_context(tc.tile_pool(name="reused", bufs=1))
         turn_ps = ctx.enter_context(tc.psum_pool(name="turn_ps", bufs=2))
-        state_ps = ctx.enter_context(tc.psum_pool(name="state_ps", bufs=3))
-        out_ps = ctx.enter_context(tc.psum_pool(name="out_ps", bufs=3))
+        state_ps = ctx.enter_context(tc.psum_pool(name="state_ps", bufs=2))
+        out_ps = ctx.enter_context(tc.psum_pool(name="out_ps", bufs=4))
 
         def sb(shape, dtype, name, offset=None):
             if offset is None:
@@ -58,9 +59,8 @@ def tile_attend_glin_q_pl_kernel(tc, kT, vT, cd, ce, doT, offs, out_0, out_1, ou
         for t in range(1, PACK):
             nc.sync.dma_start(out=v_pool[t][:], in_=v_rows[:, t, :])
         for j in range(PACK):
-            if j == PACK - 1:
-                nc.sync.dma_start(out=do_raw[:], in_=doT.rearrange("(p t) r -> p t r", t=PACK))
             nc.sync.dma_start(out=k_pool[j][:], in_=k_rows[:, j, :])
+        nc.sync.dma_start(out=do_raw[:], in_=doT.rearrange("(p t) r -> p t r", t=PACK))
 
         ident = sb([P, P], F32, "ident")
         make_identity(nc, ident[:])
@@ -165,13 +165,6 @@ def tile_attend_glin_q_pl_kernel(tc, kT, vT, cd, ce, doT, offs, out_0, out_1, ou
         for t in range(PACK):
             group(v_grouped[:, t * P * PACK : (t + 1) * P * PACK], gather_and_turn(v_pool[t], "v%d" % t))
 
-        y = sb([P, PACK, R], F32, "y")
-        out_rows = out_0.rearrange("(m j) r -> m j r", j=PACK)
-
-        def hand_out(j, acc):
-            nc.scalar.copy(y[:, j, :], acc[:])
-            nc.sync.dma_start(out=out_rows[:, j, :], in_=y[:, j, :])
-
         k0 = sb([P, P * PACK], BF16, "k0_grouped")
         group(k0, gather_and_turn(k_pool[0], "k0"))
         v_codes, v_scales = quantize(v_grouped[:], E4M3, "v", k_bytes(0))
@@ -179,14 +172,12 @@ def tile_attend_glin_q_pl_kernel(tc, kT, vT, cd, ce, doT, offs, out_0, out_1, ou
         group(k1, gather_and_turn(k_pool[1], "k1"))
         state0 = first_product(*quantize(k0[:], E4M3, "k0", k_bytes(1)))
         k2 = sb([P, P * PACK], BF16, "k2_grouped")
-        group(k2, gather_and_turn(k_pool[2], "k2", k_bytes(PACK + 1)))
-        do_grouped = sb([P, R * PACK], BF16, "do_grouped", k_bytes(PACK + 1))
-        for lo in range(0, R, 128):
-            interleave(nc.scalar.copy, do_grouped, do_raw, lo, lo + 128)
+        group(k2, gather_and_turn(k_pool[2], "k2"))
         state1 = first_product(*quantize(k1[:], E4M3, "k1", k_bytes(2)))
-        s0 = quantize(weigh(0, state0, k_bytes(2) + 1024)[:], E4M3, "s0")
-        s1_grouped = weigh(1, state1)
-        k2_q = quantize(k2[:], E4M3, "k2")
+        s0_grouped = weigh(0, state0, k_bytes(2) + 1024)
+        k3 = sb([P, P * PACK], BF16, "k3_grouped")
+        group(k3, gather_and_turn(k_pool[3], "k3"))
+        k2_q = quantize(k2[:], E4M3, "k2", k_bytes(3))
         state2 = first_product(*k2_q)
         warm = out_ps.tile([P, R], F32, name="acc")
         for w in range(2):
@@ -199,38 +190,42 @@ def tile_attend_glin_q_pl_kernel(tc, kT, vT, cd, ce, doT, offs, out_0, out_1, ou
                 start=True,
                 stop=True,
             )
-        turned3 = gather_and_turn(k_pool[3], "k3")
-        do_codes, do_scales = quantize(do_grouped[:], E5M2, "do", k_bytes(3))
-        s2_grouped = weigh(2, state2, k_bytes(3) + 2048)
-        k3 = sb([P, P * PACK], BF16, "k3_grouped", k_bytes(PACK))
-        group(k3, turned3)
-        hand_out(0, multiply(*s0))
-        whole3 = first_product(*quantize(k3[:], E4M3, "k3"))
-        state3 = [whole3[:, :, lo : lo + HALF] for lo in (0, HALF)]
-        hand_out(1, multiply(*quantize(s1_grouped[:], E4M3, "s1", k_bytes(PACK))))
-        hand_out(2, multiply(*quantize(s2_grouped[:], E4M3, "s2", k_bytes(PACK) + 512)))
-        s3_grouped = sb([P, P * PACK], BF16, "s3_grouped")
+        s0 = quantize(s0_grouped[:], E4M3, "s0", k_bytes(3) + 512)
+        s1 = quantize(weigh(1, state1, k_bytes(3) + 1024)[:], E4M3, "s1")
+        k3_q = quantize(k3[:], E4M3, "k3")
+        state3 = first_product(*k3_q)
+        s2_grouped = weigh(2, state2)
+        do_grouped = sb([P, R * PACK], BF16, "do_grouped", k_bytes(PACK + 1))
+        do_codes = sb([P, R], U32, "do_codes")
+        do_scales = sb([P, R], U8, "do_scales")
+        interleave(nc.scalar.copy, do_grouped, do_raw, 0, 256)
+        interleave(nc.scalar.copy, do_grouped, do_raw, 256, SCALAR_COLUMNS)
+        interleave(nc.vector.tensor_copy, do_grouped, do_raw, SCALAR_COLUMNS, R)
+        quantize_columns(do_codes, do_scales, do_grouped, E5M2, 0, 256)
+        quantize_columns(do_codes, do_scales, do_grouped, E5M2, 256, R)
+        s2 = quantize(s2_grouped[:], E4M3, "s2", k_bytes(PACK + 1) + 1024)
+        acc0, acc1, acc2 = multiply(*s0), multiply(*s1), multiply(*s2)
+        s3_grouped = sb([P, P * PACK], BF16, "s3_grouped", k_bytes(PACK + 1))
         s3_codes = sb([P, P], U32, "s3_codes")
         s3_scales = sb([P, P], U8, "s3_scales")
-        for h in range(2):
-            weigh_columns(s3_grouped, 3, state3[h], h * HALF, (h + 1) * HALF)
+        for lo in (0, HALF):
+            weigh_columns(s3_grouped, 3, state3[:, :, lo : lo + HALF], lo, lo + HALF)
         for lo in (0, HALF):
             quantize_columns(s3_codes, s3_scales, s3_grouped, E4M3, lo, lo + HALF)
-        acc = multiply(s3_codes, s3_scales)
+        acc3 = multiply(s3_codes, s3_scales)
+
+        y = sb([P, PACK, R], F32, "y")
+        out_rows = out_0.rearrange("(m j) r -> m j r", j=PACK)
+        nc.scalar.copy(y[:, 0, :], acc0[:])
+        nc.sync.dma_start(out=out_rows[:, 0, :], in_=y[:, 0, :])
+        nc.scalar.copy(y[:, 1, :], acc1[:])
+        nc.vector.tensor_copy(y[:, 2, :], acc2[:])
+        nc.sync.dma_start(out=out_rows[:, 1:3, :], in_=y[:, 1:3, :])
 
         y_grouped = sb([P, R * PACK], BF16, "y_grouped")
-        y_places = y_grouped[:].rearrange("p (r j) -> p r j", j=PACK)
-
-        def pair_of_places(engine_copy, first, lo, hi):
-            engine_copy(
-                y_places[:, lo:hi, first : first + 2].rearrange("p (c i) t -> p c t i", i=4),
-                y[:, first : first + 2, lo:hi].rearrange("p t (c i) -> p c t i", i=4),
-            )
-
-        pair_of_places(nc.vector.tensor_copy, 0, 0, R)
         for lo in range(0, R, 128):
-            nc.scalar.copy(y[:, 3, lo : lo + 128], acc[:, lo : lo + 128])
-            pair_of_places(nc.scalar.copy if lo == 384 else nc.vector.tensor_copy, 2, lo, lo + 128)
+            nc.scalar.copy(y[:, 3, lo : lo + 128], acc3[:, lo : lo + 128])
+            interleave(nc.scalar.copy if lo == 384 else nc.vector.tensor_copy, y_grouped, y, lo, lo + 128)
         nc.sync.dma_start(out=out_rows[:, 3, :], in_=y[:, 3, :])
         y_codes = sb([P, R], U32, "y_codes")
         y_scales = sb([P, R], U8, "y_scales")

@@ -20,7 +20,6 @@ T = 2048
 SLOTS = 512
 R = 512
 HALF = P // 2
-SCALAR_COLUMNS = 352
 
 FLOPS = 2 * D * D * SLOTS + 2 * D * D * R
 BYTES = 4 * (2 * D * T + D + D + D * R + D * R) + 2 * P * SLOTS // 16 + D * R + D * R // 32
@@ -194,39 +193,53 @@ def tile_attend_glin_q_pl_kernel(tc, kT, vT, cd, ce, doT, offs, out_0, out_1, ou
         s1 = quantize(weigh(1, state1, k_bytes(3) + 1024)[:], E4M3, "s1")
         k3_q = quantize(k3[:], E4M3, "k3")
         state3 = first_product(*k3_q)
-        s2_grouped = weigh(2, state2)
-        do_grouped = sb([P, R * PACK], BF16, "do_grouped", k_bytes(PACK + 1))
         do_codes = sb([P, R], U32, "do_codes")
         do_scales = sb([P, R], U8, "do_scales")
-        interleave(nc.scalar.copy, do_grouped, do_raw, 0, 256)
-        interleave(nc.scalar.copy, do_grouped, do_raw, 256, SCALAR_COLUMNS)
-        interleave(nc.vector.tensor_copy, do_grouped, do_raw, SCALAR_COLUMNS, R)
-        quantize_columns(do_codes, do_scales, do_grouped, E5M2, 0, 256)
-        quantize_columns(do_codes, do_scales, do_grouped, E5M2, 256, R)
-        s2 = quantize(s2_grouped[:], E4M3, "s2", k_bytes(PACK + 1) + 1024)
-        acc0, acc1, acc2 = multiply(*s0), multiply(*s1), multiply(*s2)
-        s3_grouped = sb([P, P * PACK], BF16, "s3_grouped", k_bytes(PACK + 1))
+
+        def group_do(engine_copy, lo, hi, offset=None):
+            grouped = sb([P, (hi - lo) * PACK], BF16, "do_grouped%d" % lo, offset)
+            interleave(engine_copy, grouped, do_raw[:, :, lo:hi], 0, hi - lo)
+            return grouped
+
+        def quantize_do(grouped, lo, hi):
+            nc.vector.quantize_mx(out=do_codes[:, lo:hi].bitcast(E5M2), scales=do_scales[:, lo:hi], in_=grouped[:])
+
+        def pair(engine_copy, grouped, planes, u, lo, hi):
+            engine_copy(
+                grouped[:, lo * PACK : hi * PACK].rearrange("p (c i t) -> p c t i", i=4, t=PACK)[:, :, 2 * u : 2 * u + 2, :],
+                planes[:, :, lo:hi].rearrange("p t (c i) -> p c t i", i=4),
+            )
+
+        do_a = group_do(nc.vector.tensor_copy, 0, 128)
+        do_b = group_do(nc.vector.tensor_copy, 128, 256)
+        do_c = group_do(nc.scalar.copy, 256, R, k_bytes(PACK))
+        quantize_do(do_a, 0, 128)
+        quantize_do(do_b, 128, 256)
+        quantize_do(do_c, 256, R)
+        acc0, acc1 = multiply(*s0), multiply(*s1)
+        s2_grouped = weigh(2, state2, k_bytes(PACK))
+        s3_grouped = sb([P, P * PACK], BF16, "s3_grouped", k_bytes(PACK) + 1024)
         s3_codes = sb([P, P], U32, "s3_codes")
         s3_scales = sb([P, P], U8, "s3_scales")
-        for lo in (0, HALF):
-            weigh_columns(s3_grouped, 3, state3[:, :, lo : lo + HALF], lo, lo + HALF)
+        weigh_columns(s3_grouped, 3, state3[:, :, 0:HALF], 0, HALF)
+        acc2 = multiply(*quantize(s2_grouped[:], E4M3, "s2"))
+        weigh_columns(s3_grouped, 3, state3[:, :, HALF:P], HALF, P)
         for lo in (0, HALF):
             quantize_columns(s3_codes, s3_scales, s3_grouped, E4M3, lo, lo + HALF)
         acc3 = multiply(s3_codes, s3_scales)
 
-        y = sb([P, PACK, R], F32, "y")
+        y01 = sb([P, 2, R], F32, "y01")
+        y23 = sb([P, 2, R], F32, "y23")
         out_rows = out_0.rearrange("(m j) r -> m j r", j=PACK)
-        nc.scalar.copy(y[:, 0, :], acc0[:])
-        nc.sync.dma_start(out=out_rows[:, 0, :], in_=y[:, 0, :])
-        nc.scalar.copy(y[:, 1, :], acc1[:])
-        nc.vector.tensor_copy(y[:, 2, :], acc2[:])
-        nc.sync.dma_start(out=out_rows[:, 1:3, :], in_=y[:, 1:3, :])
-
-        y_grouped = sb([P, R * PACK], BF16, "y_grouped")
+        for j, (plane, acc) in enumerate(((y01[:, 0, :], acc0), (y01[:, 1, :], acc1), (y23[:, 0, :], acc2))):
+            nc.scalar.copy(plane, acc[:])
+            nc.sync.dma_start(out=out_rows[:, j, :], in_=plane)
+        y_grouped = sb([P, R * PACK], BF16, "y_grouped", k_bytes(PACK) + 1024)
+        pair(nc.vector.tensor_copy, y_grouped, y01, 0, 0, R)
         for lo in range(0, R, 128):
-            nc.scalar.copy(y[:, 3, lo : lo + 128], acc3[:, lo : lo + 128])
-            interleave(nc.scalar.copy if lo == 384 else nc.vector.tensor_copy, y_grouped, y, lo, lo + 128)
-        nc.sync.dma_start(out=out_rows[:, 3, :], in_=y[:, 3, :])
+            nc.scalar.copy(y23[:, 1, lo : lo + 128], acc3[:, lo : lo + 128])
+            pair(nc.scalar.copy if lo == 384 else nc.vector.tensor_copy, y_grouped, y23, 1, lo, lo + 128)
+        nc.sync.dma_start(out=out_rows[:, 3, :], in_=y23[:, 1, :])
         y_codes = sb([P, R], U32, "y_codes")
         y_scales = sb([P, R], U8, "y_scales")
         words = out_1[0].rearrange("p c l -> p (c l)").bitcast(I32)

@@ -178,17 +178,6 @@ def tile_attend_glin_q_pl_kernel(tc, kT, vT, cd, ce, doT, offs, out_0, out_1, ou
         group(k3, gather_and_turn(k_pool[3], "k3"))
         k2_q = quantize(k2[:], E4M3, "k2", k_bytes(3))
         state2 = first_product(*k2_q)
-        warm = out_ps.tile([P, R], F32, name="acc")
-        for w in range(2):
-            nc.tensor.matmul_mx(
-                out=warm[:],
-                lhsT=k2_q[0][:].bitcast(E4M3),
-                lhsT_scale=k2_q[1][:],
-                rhs=v_codes[:].bitcast(E4M3),
-                rhs_scale=v_scales[:],
-                start=True,
-                stop=True,
-            )
         s0 = quantize(s0_grouped[:], E4M3, "s0", k_bytes(3) + 512)
         s1 = quantize(weigh(1, state1, k_bytes(3) + 1024)[:], E4M3, "s1")
         k3_q = quantize(k3[:], E4M3, "k3")

@@ -12,6 +12,7 @@ U8 = mybir.dt.uint8
 E4M3 = mybir.dt.float8_e4m3fn_x4
 E5M2 = mybir.dt.float8_e5m2_x4
 MULT = mybir.AluOpType.mult
+COPY = mybir.ActivationFunctionType.Copy
 
 P = 128
 PACK = 4
@@ -20,6 +21,8 @@ T = 2048
 SLOTS = 512
 R = 512
 HALF = P // 2
+VECTOR_SLOTS = 288
+VECTOR_DO = 256
 
 FLOPS = 2 * D * D * SLOTS + 2 * D * D * R
 BYTES = 4 * (2 * D * T + D + D + D * R + D * R) + 2 * P * SLOTS // 16 + D * R + D * R // 32
@@ -42,8 +45,15 @@ def tile_attend_glin_q_pl_kernel(tc, kT, vT, cd, ce, doT, offs, out_0, out_1, ou
         def k_bytes(j):
             return j * T * 4
 
+        def v_bytes(t):
+            return (PACK + t) * T * 4
+
+        spare = 2 * PACK * T * 4
+
+        picked_bytes = spare + R * PACK * 2
+
         offsets = keep.tile([P, SLOTS // 16], U16, name="offsets")
-        v_pool = [sb([P, T], F32, "v_pool%d" % t) for t in range(PACK)]
+        v_pool = [sb([P, T], F32, "v_pool%d" % t, v_bytes(t)) for t in range(PACK)]
         k_pool = [sb([P, T], F32, "k_pool%d" % j, k_bytes(j)) for j in range(PACK)]
         do_raw = sb([P, PACK, R], F32, "do_raw")
         rows = sb([P, D], F32, "rows")
@@ -73,8 +83,9 @@ def tile_attend_glin_q_pl_kernel(tc, kT, vT, cd, ce, doT, offs, out_0, out_1, ou
         cd_rows = state_ps.tile([P, PACK, P], F32, name="state")
         for j in range(PACK):
             nc.tensor.transpose(cd_rows[:, j, :], cd_col[:, j : j + 1].to_broadcast([P, P]), ident[:])
-        factor = [sb([P, P, PACK], F32, "factor%d" % j) for j in range(PACK)]
-        for j in range(PACK):
+        factor = [sb([P, P, PACK], F32, "factor%d" % j, v_bytes(j)) for j in range(PACK)]
+
+        def make_factor(j):
             nc.vector.tensor_tensor(
                 factor[j][:],
                 cd_rows[:, j, :].unsqueeze(2).to_broadcast([P, P, PACK]),
@@ -82,12 +93,12 @@ def tile_attend_glin_q_pl_kernel(tc, kT, vT, cd, ce, doT, offs, out_0, out_1, ou
                 MULT,
             )
 
-        picks = {}
-
-        def gather_and_turn(pool, name, offset=None):
-            picked = sb([P, SLOTS], BF16, name + "_picked", offset)
-            picks[name] = picked
-            nc.vector.tensor_copy(picked[:], pool[:].indirect(offsets[:]))
+        def gather_and_turn(pool, name, cut=VECTOR_SLOTS):
+            picked = sb([P, SLOTS], BF16, name + "_picked", picked_bytes if name in ("k2", "k3") else None)
+            if cut > 0:
+                nc.vector.tensor_copy(picked[:, :cut], pool[:].indirect(offsets[:, : cut // 16]))
+            if cut < SLOTS:
+                nc.scalar.activation(picked[:, cut:], pool[:].indirect(offsets[:, cut // 16 :]), COPY)
             pairs = picked[:].bitcast(F32)
             turned = turn_ps.tile([P, 2, P], F32, name="turned")
             for u in range(2):
@@ -140,18 +151,17 @@ def tile_attend_glin_q_pl_kernel(tc, kT, vT, cd, ce, doT, offs, out_0, out_1, ou
             weigh_columns(s_grouped, j, state[:], 0, P)
             return s_grouped
 
-        def multiply(s_codes, s_scales):
-            acc = out_ps.tile([P, R], F32, name="acc")
+        def multiply(acc, s_q, lo, hi):
+            s_codes, s_scales = s_q
             nc.tensor.matmul_mx(
-                out=acc[:],
+                out=acc,
                 lhsT=s_codes[:].bitcast(E4M3),
                 lhsT_scale=s_scales[:],
-                rhs=do_codes[:].bitcast(E5M2),
-                rhs_scale=do_scales[:],
+                rhs=do_codes[:, lo:hi].bitcast(E5M2),
+                rhs_scale=do_scales[:, lo:hi],
                 start=True,
                 stop=True,
             )
-            return acc
 
         def quantize_columns(codes, scales, grouped, fmt, lo, hi):
             nc.vector.quantize_mx(
@@ -162,36 +172,33 @@ def tile_attend_glin_q_pl_kernel(tc, kT, vT, cd, ce, doT, offs, out_0, out_1, ou
 
         v_grouped = sb([P, D * PACK], BF16, "v_grouped")
         for t in range(PACK):
-            group(v_grouped[:, t * P * PACK : (t + 1) * P * PACK], gather_and_turn(v_pool[t], "v%d" % t))
+            group(v_grouped[:, t * P * PACK : (t + 1) * P * PACK], gather_and_turn(v_pool[t], "v%d" % t, SLOTS))
+            make_factor(t)
 
-        k0 = sb([P, P * PACK], BF16, "k0_grouped")
-        group(k0, gather_and_turn(k_pool[0], "k0"))
+        def grouped_keys(j, turned, offset=None):
+            k_grouped = sb([P, P * PACK], BF16, "k%d_grouped" % j, offset)
+            group(k_grouped, turned)
+            return k_grouped
+
+        k0 = grouped_keys(0, gather_and_turn(k_pool[0], "k0", SLOTS))
         v_codes, v_scales = quantize(v_grouped[:], E4M3, "v", k_bytes(0))
-        k1 = sb([P, P * PACK], BF16, "k1_grouped")
-        group(k1, gather_and_turn(k_pool[1], "k1"))
+        k1_turned = gather_and_turn(k_pool[1], "k1", SLOTS)
         state0 = first_product(*quantize(k0[:], E4M3, "k0", k_bytes(1)))
-        k2 = sb([P, P * PACK], BF16, "k2_grouped")
-        group(k2, gather_and_turn(k_pool[2], "k2"))
-        state1 = first_product(*quantize(k1[:], E4M3, "k1", k_bytes(2)))
+        k2_turned = gather_and_turn(k_pool[2], "k2")
+        k1 = grouped_keys(1, k1_turned, k_bytes(2))
+        k2 = grouped_keys(2, k2_turned, k_bytes(1) + 1024)
         s0_grouped = weigh(0, state0, k_bytes(2) + 1024)
-        k3 = sb([P, P * PACK], BF16, "k3_grouped")
-        group(k3, gather_and_turn(k_pool[3], "k3"))
-        k2_q = quantize(k2[:], E4M3, "k2", k_bytes(3))
+        state1 = first_product(*quantize(k1[:], E4M3, "k1"))
+        s0 = quantize(s0_grouped[:], E4M3, "s0")
+        k2_q = quantize(k2[:], E4M3, "k2")
         state2 = first_product(*k2_q)
-        s0 = quantize(s0_grouped[:], E4M3, "s0", k_bytes(3) + 512)
-        s1 = quantize(weigh(1, state1, k_bytes(3) + 1024)[:], E4M3, "s1")
+        k3 = grouped_keys(3, gather_and_turn(k_pool[3], "k3", 224))
+        s1_grouped = weigh(1, state1, k_bytes(3) + 4096)
+        s2_grouped = weigh(2, state2, k_bytes(3) + 5120)
         k3_q = quantize(k3[:], E4M3, "k3")
         state3 = first_product(*k3_q)
         do_codes = sb([P, R], U32, "do_codes")
         do_scales = sb([P, R], U8, "do_scales")
-
-        def group_do(engine_copy, lo, hi, offset=None):
-            grouped = sb([P, (hi - lo) * PACK], BF16, "do_grouped%d" % lo, offset)
-            interleave(engine_copy, grouped, do_raw[:, :, lo:hi], 0, hi - lo)
-            return grouped
-
-        def quantize_do(grouped, lo, hi):
-            nc.vector.quantize_mx(out=do_codes[:, lo:hi].bitcast(E5M2), scales=do_scales[:, lo:hi], in_=grouped[:])
 
         def pair(engine_copy, grouped, planes, u, lo, hi):
             engine_copy(
@@ -199,35 +206,58 @@ def tile_attend_glin_q_pl_kernel(tc, kT, vT, cd, ce, doT, offs, out_0, out_1, ou
                 planes[:, :, lo:hi].rearrange("p t (c i) -> p c t i", i=4),
             )
 
-        do_a = group_do(nc.vector.tensor_copy, 0, 128)
-        do_b = group_do(nc.vector.tensor_copy, 128, 256)
-        do_c = group_do(nc.scalar.copy, 256, R, k_bytes(PACK))
-        quantize_do(do_a, 0, 128)
-        quantize_do(do_b, 128, 256)
-        quantize_do(do_c, 256, R)
-        acc0, acc1 = multiply(*s0), multiply(*s1)
-        s2_grouped = weigh(2, state2, k_bytes(PACK))
-        s3_grouped = sb([P, P * PACK], BF16, "s3_grouped", k_bytes(PACK) + 1024)
-        s3_codes = sb([P, P], U32, "s3_codes")
-        s3_scales = sb([P, P], U8, "s3_scales")
-        weigh_columns(s3_grouped, 3, state3[:, :, 0:HALF], 0, HALF)
-        acc2 = multiply(*quantize(s2_grouped[:], E4M3, "s2"))
-        weigh_columns(s3_grouped, 3, state3[:, :, HALF:P], HALF, P)
-        for lo in (0, HALF):
-            quantize_columns(s3_codes, s3_scales, s3_grouped, E4M3, lo, lo + HALF)
-        acc3 = multiply(s3_codes, s3_scales)
+        def group_do(grouped, base, engine_copy, lo, hi):
+            interleave(engine_copy, grouped, do_raw[:, :, base:], lo - base, hi - base)
 
+        def quantize_do(grouped, lo, hi):
+            nc.vector.quantize_mx(out=do_codes[:, lo:hi].bitcast(E5M2), scales=do_scales[:, lo:hi], in_=grouped[:])
+
+        mid = R // 2
         y01 = sb([P, 2, R], F32, "y01")
         y23 = sb([P, 2, R], F32, "y23")
         out_rows = out_0.rearrange("(m j) r -> m j r", j=PACK)
-        for j, (plane, acc) in enumerate(((y01[:, 0, :], acc0), (y01[:, 1, :], acc1), (y23[:, 0, :], acc2))):
-            nc.scalar.copy(plane, acc[:])
-            nc.sync.dma_start(out=out_rows[:, j, :], in_=plane)
-        y_grouped = sb([P, R * PACK], BF16, "y_grouped", k_bytes(PACK) + 1024)
-        pair(nc.vector.tensor_copy, y_grouped, y01, 0, 0, R)
-        for lo in range(0, R, 128):
-            nc.scalar.copy(y23[:, 1, lo : lo + 128], acc3[:, lo : lo + 128])
-            pair(nc.scalar.copy if lo == 384 else nc.vector.tensor_copy, y_grouped, y23, 1, lo, lo + 128)
+        y_grouped = sb([P, R * PACK], BF16, "y_grouped", k_bytes(3))
+
+        def product(pool, name, s_q, plane, lo, hi, engine_copy):
+            acc = pool.tile([P, hi - lo], F32, name=name)
+            multiply(acc[:], s_q, lo, hi)
+            engine_copy(plane[:, lo:hi], acc[:])
+
+        do_a = sb([P, 128 * PACK], BF16, "do_a", spare + 2048)
+        do_b = sb([P, 128 * PACK], BF16, "do_b", spare + 3072)
+        do_c = sb([P, 256 * PACK], BF16, "do_c", spare)
+        group_do(do_a, 0, nc.vector.tensor_copy, 0, 128)
+        group_do(do_b, 128, nc.vector.tensor_copy, 128, 256)
+        group_do(do_c, 256, nc.scalar.copy, VECTOR_DO, R)
+        quantize_do(do_a, 0, 128)
+        quantize_do(do_b, 128, 256)
+        product(out_ps, "acc", s0, y01[:, 0, :], 0, mid, nc.scalar.copy)
+        quantize_do(do_c, 256, R)
+        s1 = quantize(s1_grouped[:], E4M3, "s1", spare + 1024)
+        s2 = quantize(s2_grouped[:], E4M3, "s2", spare + 1536)
+        product(out_ps, "acc", s0, y01[:, 0, :], mid, R, nc.scalar.copy)
+        nc.sync.dma_start(out=out_rows[:, 0, :], in_=y01[:, 0, :])
+        acc1 = out_ps.tile([P, R], F32, name="acc")
+        multiply(acc1[:], s1, 0, R)
+        for lo in (0, mid):
+            nc.scalar.copy(y01[:, 1, lo : lo + mid], acc1[:, lo : lo + mid])
+        nc.sync.dma_start(out=out_rows[:, 1, :], in_=y01[:, 1, :])
+        product(out_ps, "acc", s2, y23[:, 0, :], 0, R, nc.scalar.copy)
+        nc.sync.dma_start(out=out_rows[:, 2, :], in_=y23[:, 0, :])
+        s3_grouped = sb([P, P * PACK], BF16, "s3_grouped", spare)
+        s3_codes = sb([P, P], U32, "s3_codes")
+        s3_scales = sb([P, P], U8, "s3_scales")
+        for lo in (0, HALF):
+            weigh_columns(s3_grouped, 3, state3[:, :, lo : lo + HALF], lo, lo + HALF)
+        for lo in (0, HALF):
+            quantize_columns(s3_codes, s3_scales, s3_grouped, E4M3, lo, lo + HALF)
+        for lo in (0, mid):
+            pair(nc.vector.tensor_copy, y_grouped, y01, 0, lo, lo + mid)
+        for lo in (0, mid):
+            product(turn_ps, "turned", (s3_codes, s3_scales), y23[:, 1, :], lo, lo + mid, nc.scalar.copy)
+        pair(nc.vector.tensor_copy, y_grouped, y23, 1, 0, mid)
+        pair(nc.vector.tensor_copy, y_grouped, y23, 1, mid, 384)
+        pair(nc.scalar.copy, y_grouped, y23, 1, 384, R)
         nc.sync.dma_start(out=out_rows[:, 3, :], in_=y23[:, 1, :])
         y_codes = sb([P, R], U32, "y_codes")
         y_scales = sb([P, R], U8, "y_scales")

@@ -21,8 +21,9 @@ T = 2048
 SLOTS = 512
 R = 512
 HALF = P // 2
-VECTOR_SLOTS = 288
-VECTOR_DO = 256
+MID = R // 2
+SHARE = 288
+LAST_SHARE = 224
 
 FLOPS = 2 * D * D * SLOTS + 2 * D * D * R
 BYTES = 4 * (2 * D * T + D + D + D * R + D * R) + 2 * P * SLOTS // 16 + D * R + D * R // 32
@@ -50,40 +51,40 @@ def tile_attend_glin_q_pl_kernel(tc, kT, vT, cd, ce, doT, offs, out_0, out_1, ou
 
         spare = 2 * PACK * T * 4
 
-        picked_bytes = spare + R * PACK * 2
-
         offsets = keep.tile([P, SLOTS // 16], U16, name="offsets")
-        v_pool = [sb([P, T], F32, "v_pool%d" % t, v_bytes(t)) for t in range(PACK)]
+        v_pool = [sb([P, 2 * T], F32, "v_pool%d" % h, v_bytes(2 * h)) for h in range(2)]
         k_pool = [sb([P, T], F32, "k_pool%d" % j, k_bytes(j)) for j in range(PACK)]
         do_raw = sb([P, PACK, R], F32, "do_raw")
         rows = sb([P, D], F32, "rows")
         nc.vector.memset(rows[:], 0.0)
 
-        v_rows = vT.rearrange("(m t) n -> m t n", t=PACK)
+        v_rows = vT.rearrange("(m h t) n -> m h (t n)", h=2, t=2)
         k_rows = kT.rearrange("(m j) n -> m j n", j=PACK)
+        do_rows = doT.rearrange("(p t) r -> p t r", t=PACK)
         nc.sync.dma_start(out=v_pool[0][:], in_=v_rows[:, 0, :])
         nc.sync.dma_start(offsets[:], offs)
         nc.sync.dma_start(out=rows[0:1, :], in_=cd.rearrange("d o -> o d"))
         nc.sync.dma_start(out=rows[1:2, :], in_=ce[0:1, :])
-        for t in range(1, PACK):
-            nc.sync.dma_start(out=v_pool[t][:], in_=v_rows[:, t, :])
+        nc.sync.dma_start(out=v_pool[1][:], in_=v_rows[:, 1, :])
         for j in range(PACK):
             nc.sync.dma_start(out=k_pool[j][:], in_=k_rows[:, j, :])
-        nc.sync.dma_start(out=do_raw[:], in_=doT.rearrange("(p t) r -> p t r", t=PACK))
+        nc.sync.dma_start(out=do_raw[:], in_=do_rows)
 
         ident = sb([P, P], F32, "ident")
         make_identity(nc, ident[:])
 
-        columns_ps = state_ps.tile([P, PACK, P], F32, name="state")
-        for j in range(PACK):
-            nc.tensor.transpose(columns_ps[:, j, :], rows[:, j::PACK], ident[:])
         columns = sb([P, 2, PACK], F32, "columns")
-        nc.scalar.copy(columns[:], columns_ps[:, :, 0:2].rearrange("p j w -> p w j"))
+        for first in (0, 2):
+            columns_ps = turn_ps.tile([P, 2, P], F32, name="turned")
+            for j in range(2):
+                nc.tensor.transpose(columns_ps[:, j, :], rows[:, first + j :: PACK], ident[:])
+            nc.scalar.copy(columns[:, :, first : first + 2], columns_ps[:, :, 0:2].rearrange("p j w -> p w j"))
         cd_col, ce_col = columns[:, 0, :], columns[:, 1, :]
         cd_rows = state_ps.tile([P, PACK, P], F32, name="state")
         for j in range(PACK):
             nc.tensor.transpose(cd_rows[:, j, :], cd_col[:, j : j + 1].to_broadcast([P, P]), ident[:])
-        factor = [sb([P, P, PACK], F32, "factor%d" % j, v_bytes(j)) for j in range(PACK)]
+        factor_bytes = [v_bytes(0), v_bytes(0) + 2048, k_bytes(0) + 2048, k_bytes(1) + 2048]
+        factor = [sb([P, P, PACK], F32, "factor%d" % j, factor_bytes[j]) for j in range(PACK)]
 
         def make_factor(j):
             nc.vector.tensor_tensor(
@@ -93,46 +94,57 @@ def tile_attend_glin_q_pl_kernel(tc, kT, vT, cd, ce, doT, offs, out_0, out_1, ou
                 MULT,
             )
 
-        def gather_and_turn(pool, name, cut=VECTOR_SLOTS):
-            picked = sb([P, SLOTS], BF16, name + "_picked", picked_bytes if name in ("k2", "k3") else None)
+        def gather_and_turn(pool, name, cut, banks=(turn_ps, "turned")):
+            picked = sb([P, SLOTS], BF16, name + "_picked")
             if cut > 0:
                 nc.vector.tensor_copy(picked[:, :cut], pool[:].indirect(offsets[:, : cut // 16]))
             if cut < SLOTS:
                 nc.scalar.activation(picked[:, cut:], pool[:].indirect(offsets[:, cut // 16 :]), COPY)
             pairs = picked[:].bitcast(F32)
-            turned = turn_ps.tile([P, 2, P], F32, name="turned")
+            turned = banks[0].tile([P, 2, P], F32, name=banks[1])
             for u in range(2):
                 nc.tensor.transpose(turned[:, u, :], pairs[:, u::2], ident[:])
             return turned
 
-        def group(grouped, turned, lo=0, hi=P):
-            nc.scalar.copy(
-                grouped[:, lo * PACK : hi * PACK].bitcast(F32).rearrange("p (m u) -> p m u", u=2),
-                turned[:, :, lo:hi].rearrange("p u m -> p m u"),
+        def gather_dealt_and_turn(window, name, banks=(turn_ps, "turned")):
+            picked = sb([P, SLOTS], BF16, name + "_picked")
+            nc.vector.tensor_copy(picked[:].rearrange("p (u m w) -> p m u w", u=2, w=2), window.indirect(offsets[:]))
+            pairs = picked[:].bitcast(F32)
+            turned = banks[0].tile([P, 2, P], F32, name=banks[1])
+            for u in range(2):
+                nc.tensor.transpose(turned[:, u, :], pairs[:, u * P : (u + 1) * P], ident[:])
+            return turned
+
+        def group(engine_copy, name, turned, offset=None):
+            grouped = sb([P, P * PACK], BF16, name + "_grouped", offset)
+            engine_copy(
+                grouped[:].bitcast(F32).rearrange("p (m u) -> p m u", u=2),
+                turned[:].rearrange("p u m -> p m u"),
+            )
+            return grouped
+
+        def quantize_columns(codes, scales, grouped, fmt, lo, hi, base=0):
+            nc.vector.quantize_mx(
+                out=codes[:, lo:hi].bitcast(fmt),
+                scales=scales[:, lo:hi],
+                in_=grouped[:, (lo - base) * PACK : (hi - base) * PACK],
             )
 
-        def quantize(grouped, fmt, name, offset=None):
-            width = grouped.shape[1] // PACK
-            codes = sb([P, width], U32, name + "_codes", offset)
-            scales = sb([P, width], U8, name + "_scales")
-            nc.vector.quantize_mx(out=codes[:].bitcast(fmt), scales=scales[:], in_=grouped)
+        def quantize(grouped, name, offset=None):
+            codes = sb([P, P], U32, name + "_codes", offset)
+            scales = sb([P, P], U8, name + "_scales")
+            quantize_columns(codes, scales, grouped, E4M3, 0, P)
             return codes, scales
 
-        def interleave(engine_copy, grouped, planes, lo, hi):
-            engine_copy(
-                grouped[:, lo * PACK : hi * PACK].rearrange("p (c i t) -> p c t i", i=4, t=PACK),
-                planes[:, :, lo:hi].rearrange("p t (c i) -> p c t i", i=4),
-            )
-
-        def first_product(k_codes, k_scales, lo=0, hi=P):
-            state = state_ps.tile([P, PACK, hi - lo], F32, name="state")
+        def first_product(k_codes, k_scales):
+            state = state_ps.tile([P, PACK, P], F32, name="state")
             for t in range(PACK):
                 nc.tensor.matmul_mx(
                     out=state[:, t, :],
-                    lhsT=v_codes[:, t * P : (t + 1) * P].bitcast(E4M3),
-                    lhsT_scale=v_scales[:, t * P : (t + 1) * P],
-                    rhs=k_codes[:, lo:hi].bitcast(E4M3),
-                    rhs_scale=k_scales[:, lo:hi],
+                    lhsT=v_q[t][0][:].bitcast(E4M3),
+                    lhsT_scale=v_q[t][1][:],
+                    rhs=k_codes[:].bitcast(E4M3),
+                    rhs_scale=k_scales[:],
                     start=True,
                     stop=True,
                 )
@@ -141,130 +153,114 @@ def tile_attend_glin_q_pl_kernel(tc, kT, vT, cd, ce, doT, offs, out_0, out_1, ou
         def weigh_columns(s_grouped, j, state, lo, hi):
             nc.vector.tensor_tensor(
                 s_grouped[:, lo * PACK : hi * PACK].rearrange("p (m t) -> p m t", t=PACK),
-                state.rearrange("p t m -> p m t"),
+                state[:, :, lo:hi].rearrange("p t m -> p m t"),
                 factor[j][:, lo:hi, :],
                 MULT,
             )
 
         def weigh(j, state, offset=None):
             s_grouped = sb([P, P * PACK], BF16, "s%d_grouped" % j, offset)
-            weigh_columns(s_grouped, j, state[:], 0, P)
+            weigh_columns(s_grouped, j, state, 0, P)
             return s_grouped
 
-        def multiply(acc, s_q, lo, hi):
-            s_codes, s_scales = s_q
+        def places(engine_copy, grouped, planes, first, lo, hi, base=0):
+            count = planes.shape[1]
+            engine_copy(
+                grouped[:, (lo - base) * PACK : (hi - base) * PACK].rearrange("p (c i t) -> p c t i", i=4, t=PACK)[
+                    :, :, first : first + count, :
+                ],
+                planes[:, :, lo:hi].rearrange("p t (c i) -> p c t i", i=4),
+            )
+
+        def multiply(pool, name, s_q, lo, hi):
+            acc = pool.tile([P, hi - lo], F32, name=name)
             nc.tensor.matmul_mx(
-                out=acc,
-                lhsT=s_codes[:].bitcast(E4M3),
-                lhsT_scale=s_scales[:],
+                out=acc[:],
+                lhsT=s_q[0][:].bitcast(E4M3),
+                lhsT_scale=s_q[1][:],
                 rhs=do_codes[:, lo:hi].bitcast(E5M2),
                 rhs_scale=do_scales[:, lo:hi],
                 start=True,
                 stop=True,
             )
+            return acc
 
-        def quantize_columns(codes, scales, grouped, fmt, lo, hi):
-            nc.vector.quantize_mx(
-                out=codes[:, lo:hi].bitcast(fmt),
-                scales=scales[:, lo:hi],
-                in_=grouped[:, lo * PACK : hi * PACK],
-            )
-
-        v_grouped = sb([P, D * PACK], BF16, "v_grouped")
-        for t in range(PACK):
-            group(v_grouped[:, t * P * PACK : (t + 1) * P * PACK], gather_and_turn(v_pool[t], "v%d" % t, SLOTS))
-            make_factor(t)
-
-        def grouped_keys(j, turned, offset=None):
-            k_grouped = sb([P, P * PACK], BF16, "k%d_grouped" % j, offset)
-            group(k_grouped, turned)
-            return k_grouped
-
-        k0 = grouped_keys(0, gather_and_turn(k_pool[0], "k0", SLOTS))
-        v_codes, v_scales = quantize(v_grouped[:], E4M3, "v", k_bytes(0))
-        k1_turned = gather_and_turn(k_pool[1], "k1", SLOTS)
-        state0 = first_product(*quantize(k0[:], E4M3, "k0", k_bytes(1)))
-        k2_turned = gather_and_turn(k_pool[2], "k2")
-        k1 = grouped_keys(1, k1_turned, k_bytes(2))
-        k2 = grouped_keys(2, k2_turned, k_bytes(1) + 1024)
+        v1 = group(nc.scalar.copy, "v1", gather_dealt_and_turn(v_pool[0][:, T:], "v1"))
+        v0 = group(nc.scalar.copy, "v0", gather_and_turn(v_pool[0], "v0", SLOTS))
+        v_q = [quantize(v0, "v0"), quantize(v1, "v1")]
+        v3_turned = gather_dealt_and_turn(v_pool[1][:, T:], "v3", (out_ps, "acc"))
+        v2_turned = gather_and_turn(v_pool[1], "v2", 0, (out_ps, "acc"))
+        k0_turned = gather_and_turn(k_pool[0], "k0", SHARE)
+        v3 = group(nc.scalar.copy, "v3", v3_turned, k_bytes(0))
+        v2 = group(nc.scalar.copy, "v2", v2_turned, k_bytes(0) + 1024)
+        for j in range(PACK - 1):
+            make_factor(j)
+        v3_q = quantize(v3, "v3")
+        v_q.extend([quantize(v2, "v2"), v3_q])
+        k1_turned = gather_and_turn(k_pool[1], "k1", SHARE)
+        k0 = group(nc.scalar.copy, "k0", k0_turned, k_bytes(1))
+        make_factor(3)
+        state0 = first_product(*quantize(k0, "k0"))
+        k2_turned = gather_and_turn(k_pool[2], "k2", SHARE)
+        k1 = group(nc.scalar.copy, "k1", k1_turned, k_bytes(2))
         s0_grouped = weigh(0, state0, k_bytes(2) + 1024)
-        state1 = first_product(*quantize(k1[:], E4M3, "k1"))
-        s0 = quantize(s0_grouped[:], E4M3, "s0")
-        k2_q = quantize(k2[:], E4M3, "k2")
+        state1 = first_product(*quantize(k1, "k1"))
+        s0 = quantize(s0_grouped, "s0")
+        k2_q = quantize(group(nc.scalar.copy, "k2", k2_turned), "k2")
         state2 = first_product(*k2_q)
-        k3 = grouped_keys(3, gather_and_turn(k_pool[3], "k3", 224))
-        s1_grouped = weigh(1, state1, k_bytes(3) + 4096)
-        s2_grouped = weigh(2, state2, k_bytes(3) + 5120)
-        k3_q = quantize(k3[:], E4M3, "k3")
+        k3_turned = gather_and_turn(k_pool[3], "k3", LAST_SHARE)
+        s1_grouped = weigh(1, state1, k_bytes(3))
+        s2_grouped = weigh(2, state2, k_bytes(3) + 1024)
+        k3_q = quantize(group(nc.scalar.copy, "k3", k3_turned), "k3")
         state3 = first_product(*k3_q)
+
         do_codes = sb([P, R], U32, "do_codes")
         do_scales = sb([P, R], U8, "do_scales")
+        do_a = sb([P, P * PACK], BF16, "do_a")
+        do_b = sb([P, P * PACK], BF16, "do_b")
+        do_c = sb([P, MID * PACK], BF16, "do_c", spare)
+        places(nc.vector.tensor_copy, do_a, do_raw[:], 0, 0, P)
+        places(nc.vector.tensor_copy, do_b, do_raw[:], 0, P, MID, P)
+        places(nc.scalar.copy, do_c, do_raw[:], 0, MID, R, MID)
+        quantize_columns(do_codes, do_scales, do_a, E5M2, 0, P)
+        quantize_columns(do_codes, do_scales, do_b, E5M2, P, MID, P)
+        quantize_columns(do_codes, do_scales, do_c, E5M2, MID, R, MID)
+        s1 = quantize(s1_grouped, "s1", spare + 1024)
+        s2 = quantize(s2_grouped, "s2", spare + 1536)
+        s3_grouped = sb([P, P * PACK], BF16, "s3_grouped", spare)
+        s3 = sb([P, P], U32, "s3_codes"), sb([P, P], U8, "s3_scales")
+        for lo in (0, HALF):
+            weigh_columns(s3_grouped, 3, state3, lo, lo + HALF)
+        for lo in (0, HALF):
+            quantize_columns(s3[0], s3[1], s3_grouped, E4M3, lo, lo + HALF)
 
-        def pair(engine_copy, grouped, planes, u, lo, hi):
-            engine_copy(
-                grouped[:, lo * PACK : hi * PACK].rearrange("p (c i t) -> p c t i", i=4, t=PACK)[:, :, 2 * u : 2 * u + 2, :],
-                planes[:, :, lo:hi].rearrange("p t (c i) -> p c t i", i=4),
-            )
-
-        def group_do(grouped, base, engine_copy, lo, hi):
-            interleave(engine_copy, grouped, do_raw[:, :, base:], lo - base, hi - base)
-
-        def quantize_do(grouped, lo, hi):
-            nc.vector.quantize_mx(out=do_codes[:, lo:hi].bitcast(E5M2), scales=do_scales[:, lo:hi], in_=grouped[:])
-
-        mid = R // 2
         y01 = sb([P, 2, R], F32, "y01")
         y23 = sb([P, 2, R], F32, "y23")
+        y_grouped = sb([P, R * PACK], BF16, "y_grouped", None)
         out_rows = out_0.rearrange("(m j) r -> m j r", j=PACK)
-        y_grouped = sb([P, R * PACK], BF16, "y_grouped", k_bytes(3))
-
-        def product(pool, name, s_q, plane, lo, hi, engine_copy):
-            acc = pool.tile([P, hi - lo], F32, name=name)
-            multiply(acc[:], s_q, lo, hi)
-            engine_copy(plane[:, lo:hi], acc[:])
-
-        do_a = sb([P, 128 * PACK], BF16, "do_a", spare + 2048)
-        do_b = sb([P, 128 * PACK], BF16, "do_b", spare + 3072)
-        do_c = sb([P, 256 * PACK], BF16, "do_c", spare)
-        group_do(do_a, 0, nc.vector.tensor_copy, 0, 128)
-        group_do(do_b, 128, nc.vector.tensor_copy, 128, 256)
-        group_do(do_c, 256, nc.scalar.copy, VECTOR_DO, R)
-        quantize_do(do_a, 0, 128)
-        quantize_do(do_b, 128, 256)
-        product(out_ps, "acc", s0, y01[:, 0, :], 0, mid, nc.scalar.copy)
-        quantize_do(do_c, 256, R)
-        s1 = quantize(s1_grouped[:], E4M3, "s1", spare + 1024)
-        s2 = quantize(s2_grouped[:], E4M3, "s2", spare + 1536)
-        product(out_ps, "acc", s0, y01[:, 0, :], mid, R, nc.scalar.copy)
+        for lo in (0, MID):
+            nc.scalar.copy(y01[:, 0, lo : lo + MID], multiply(out_ps, "acc", s0, lo, lo + MID)[:])
         nc.sync.dma_start(out=out_rows[:, 0, :], in_=y01[:, 0, :])
-        acc1 = out_ps.tile([P, R], F32, name="acc")
-        multiply(acc1[:], s1, 0, R)
-        for lo in (0, mid):
-            nc.scalar.copy(y01[:, 1, lo : lo + mid], acc1[:, lo : lo + mid])
+        acc1 = multiply(out_ps, "acc", s1, 0, R)
+        for lo in (0, MID):
+            nc.scalar.copy(y01[:, 1, lo : lo + MID], acc1[:, lo : lo + MID])
         nc.sync.dma_start(out=out_rows[:, 1, :], in_=y01[:, 1, :])
-        product(out_ps, "acc", s2, y23[:, 0, :], 0, R, nc.scalar.copy)
+        nc.scalar.copy(y23[:, 0, :], multiply(out_ps, "acc", s2, 0, R)[:])
         nc.sync.dma_start(out=out_rows[:, 2, :], in_=y23[:, 0, :])
-        s3_grouped = sb([P, P * PACK], BF16, "s3_grouped", spare)
-        s3_codes = sb([P, P], U32, "s3_codes")
-        s3_scales = sb([P, P], U8, "s3_scales")
-        for lo in (0, HALF):
-            weigh_columns(s3_grouped, 3, state3[:, :, lo : lo + HALF], lo, lo + HALF)
-        for lo in (0, HALF):
-            quantize_columns(s3_codes, s3_scales, s3_grouped, E4M3, lo, lo + HALF)
-        for lo in (0, mid):
-            pair(nc.vector.tensor_copy, y_grouped, y01, 0, lo, lo + mid)
-        for lo in (0, mid):
-            product(turn_ps, "turned", (s3_codes, s3_scales), y23[:, 1, :], lo, lo + mid, nc.scalar.copy)
-        pair(nc.vector.tensor_copy, y_grouped, y23, 1, 0, mid)
-        pair(nc.vector.tensor_copy, y_grouped, y23, 1, mid, 384)
-        pair(nc.scalar.copy, y_grouped, y23, 1, 384, R)
+        for lo in (0, MID):
+            places(nc.vector.tensor_copy, y_grouped, y01[:], 0, lo, lo + MID)
+        for lo in (0, MID):
+            nc.scalar.copy(y23[:, 1, lo : lo + MID], multiply(turn_ps, "turned", s3, lo, lo + MID)[:])
+        places(nc.vector.tensor_copy, y_grouped, y23[:], 2, 0, MID)
+        places(nc.vector.tensor_copy, y_grouped, y23[:], 2, MID, 384)
+        places(nc.scalar.copy, y_grouped, y23[:], 2, 384, R)
         nc.sync.dma_start(out=out_rows[:, 3, :], in_=y23[:, 1, :])
         y_codes = sb([P, R], U32, "y_codes")
         y_scales = sb([P, R], U8, "y_scales")
         words = out_1[0].rearrange("p c l -> p (c l)").bitcast(I32)
-        for lo in (0, 256):
-            quantize_columns(y_codes, y_scales, y_grouped, E4M3, lo, lo + 256)
-            nc.sync.dma_start(out=words[:, lo : lo + 256], in_=y_codes[:, lo : lo + 256].bitcast(I32))
+        for lo in (0, MID):
+            quantize_columns(y_codes, y_scales, y_grouped, E4M3, lo, lo + MID)
+            nc.sync.dma_start(out=words[:, lo : lo + MID], in_=y_codes[:, lo : lo + MID].bitcast(I32))
         for q in range(4):
             queue = nc.sync if q == 3 else nc.scalar
             queue.dma_start(

@@ -214,6 +214,18 @@ def tile_attend_glin_q_pl_kernel(tc, kT, vT, cd, ce, doT, offs, out_0, out_1, ou
         k3_q = quantize(group(nc.scalar.copy, "k3", k3_turned), "k3")
         state3 = first_product(*k3_q)
 
+        warm = out_ps.tile([P, PACK - 1, P], F32, name="acc")
+        for t in range(PACK - 1):
+            nc.tensor.matmul_mx(
+                out=warm[:, t, :],
+                lhsT=v_q[t][0][:].bitcast(E4M3),
+                lhsT_scale=v_q[t][1][:],
+                rhs=k3_q[0][:].bitcast(E4M3),
+                rhs_scale=k3_q[1][:],
+                start=True,
+                stop=True,
+            )
+
         do_codes = sb([P, R], U32, "do_codes")
         do_scales = sb([P, R], U8, "do_scales")
         do_a = sb([P, P * PACK], BF16, "do_a")

@@ -54,7 +54,7 @@ def tile_attend_glin_q_pl_kernel(tc, kT, vT, cd, ce, doT, offs, out_0, out_1, ou
         offsets = keep.tile([P, SLOTS // 16], U16, name="offsets")
         v_pool = [sb([P, 2 * T], F32, "v_pool%d" % h, v_bytes(2 * h)) for h in range(2)]
         k_pool = [sb([P, T], F32, "k_pool%d" % j, k_bytes(j)) for j in range(PACK)]
-        do_raw = sb([P, PACK, R], F32, "do_raw")
+        do_raw = sb([P, PACK, R], F32, "do_raw", spare)
         rows = sb([P, D], F32, "rows")
         nc.vector.memset(rows[:], 0.0)
 
@@ -230,7 +230,7 @@ def tile_attend_glin_q_pl_kernel(tc, kT, vT, cd, ce, doT, offs, out_0, out_1, ou
         do_scales = sb([P, R], U8, "do_scales")
         do_a = sb([P, P * PACK], BF16, "do_a")
         do_b = sb([P, P * PACK], BF16, "do_b")
-        do_c = sb([P, MID * PACK], BF16, "do_c", spare)
+        do_c = sb([P, MID * PACK], BF16, "do_c")
         places(nc.vector.tensor_copy, do_a, do_raw[:], 0, 0, P)
         places(nc.vector.tensor_copy, do_b, do_raw[:], 0, P, MID, P)
         places(nc.scalar.copy, do_c, do_raw[:], 0, MID, R, MID)

@@ -23,7 +23,7 @@ R = 512
 HALF = P // 2
 MID = R // 2
 SHARE = 288
-LAST_SHARE = 224
+LAST_SHARE = 160
 
 FLOPS = 2 * D * D * SLOTS + 2 * D * D * R
 BYTES = 4 * (2 * D * T + D + D + D * R + D * R) + 2 * P * SLOTS // 16 + D * R + D * R // 32

@@ -23,7 +23,9 @@ R = 512
 HALF = P // 2
 MID = R // 2
 SHARE = 288
-LAST_SHARE = 160
+K2_SHARE = 192
+LAST_SHARE = 256
+DO_SPLIT = 192
 
 FLOPS = 2 * D * D * SLOTS + 2 * D * D * R
 BYTES = 4 * (2 * D * T + D + D + D * R + D * R) + 2 * P * SLOTS // 16 + D * R + D * R // 32
@@ -201,18 +203,8 @@ def tile_attend_glin_q_pl_kernel(tc, kT, vT, cd, ce, doT, offs, out_0, out_1, ou
         k0 = group(nc.scalar.copy, "k0", k0_turned, k_bytes(1))
         make_factor(3)
         state0 = first_product(*quantize(k0, "k0"))
-        k2_turned = gather_and_turn(k_pool[2], "k2", SHARE)
-        k1 = group(nc.scalar.copy, "k1", k1_turned, k_bytes(2))
-        s0_grouped = weigh(0, state0, k_bytes(2) + 1024)
-        state1 = first_product(*quantize(k1, "k1"))
-        s0 = quantize(s0_grouped, "s0")
-        k2_q = quantize(group(nc.scalar.copy, "k2", k2_turned), "k2")
-        state2 = first_product(*k2_q)
-        k3_turned = gather_and_turn(k_pool[3], "k3", LAST_SHARE)
-        s1_grouped = weigh(1, state1, k_bytes(3))
-        s2_grouped = weigh(2, state2, k_bytes(3) + 1024)
-        k3_q = quantize(group(nc.scalar.copy, "k3", k3_turned), "k3")
-        state3 = first_product(*k3_q)
+        k1_q = quantize(group(nc.scalar.copy, "k1", k1_turned), "k1")
+        state1 = first_product(*k1_q)
 
         warm = out_ps.tile([P, PACK - 1, P], F32, name="acc")
         for t in range(PACK - 1):
@@ -220,25 +212,37 @@ def tile_attend_glin_q_pl_kernel(tc, kT, vT, cd, ce, doT, offs, out_0, out_1, ou
                 out=warm[:, t, :],
                 lhsT=v_q[t][0][:].bitcast(E4M3),
                 lhsT_scale=v_q[t][1][:],
-                rhs=k3_q[0][:].bitcast(E4M3),
-                rhs_scale=k3_q[1][:],
+                rhs=k1_q[0][:].bitcast(E4M3),
+                rhs_scale=k1_q[1][:],
                 start=True,
                 stop=True,
             )
 
+        k2_turned = gather_and_turn(k_pool[2], "k2", K2_SHARE)
+        s0_grouped = weigh(0, state0, k_bytes(2))
+        s0 = quantize(s0_grouped, "s0")
+        k3_turned = gather_and_turn(k_pool[3], "k3", LAST_SHARE)
+        k2 = group(nc.scalar.copy, "k2", k2_turned, k_bytes(3))
+        s1_grouped = weigh(1, state1, k_bytes(3) + 1024)
+        state2 = first_product(*quantize(k2, "k2"))
+        s1 = quantize(s1_grouped, "s1")
+        k3_q = quantize(group(nc.scalar.copy, "k3", k3_turned), "k3")
+        state3 = first_product(*k3_q)
+
         do_codes = sb([P, R], U32, "do_codes")
         do_scales = sb([P, R], U8, "do_scales")
-        do_a = sb([P, P * PACK], BF16, "do_a")
+        do_a = sb([P, P * PACK], BF16, "do_a", k_bytes(0) + 4096)
         do_b = sb([P, P * PACK], BF16, "do_b")
         do_c = sb([P, MID * PACK], BF16, "do_c")
         places(nc.vector.tensor_copy, do_a, do_raw[:], 0, 0, P)
-        places(nc.vector.tensor_copy, do_b, do_raw[:], 0, P, MID, P)
+        places(nc.vector.tensor_copy, do_b, do_raw[:], 0, P, DO_SPLIT, P)
+        places(nc.scalar.copy, do_b, do_raw[:], 0, DO_SPLIT, MID, P)
         places(nc.scalar.copy, do_c, do_raw[:], 0, MID, R, MID)
         quantize_columns(do_codes, do_scales, do_a, E5M2, 0, P)
         quantize_columns(do_codes, do_scales, do_b, E5M2, P, MID, P)
+        s2_grouped = weigh(2, state2, k_bytes(0) + 4096)
         quantize_columns(do_codes, do_scales, do_c, E5M2, MID, R, MID)
-        s1 = quantize(s1_grouped, "s1", spare + 1024)
-        s2 = quantize(s2_grouped, "s2", spare + 1536)
+        s2 = quantize(s2_grouped, "s2")
         s3_grouped = sb([P, P * PACK], BF16, "s3_grouped", spare)
         s3 = sb([P, P], U32, "s3_codes"), sb([P, P], U8, "s3_scales")
         for lo in (0, HALF):
@@ -248,15 +252,13 @@ def tile_attend_glin_q_pl_kernel(tc, kT, vT, cd, ce, doT, offs, out_0, out_1, ou
 
         y01 = sb([P, 2, R], F32, "y01")
         y23 = sb([P, 2, R], F32, "y23")
-        y_grouped = sb([P, R * PACK], BF16, "y_grouped", None)
+        y_grouped = sb([P, R * PACK], BF16, "y_grouped", spare)
         out_rows = out_0.rearrange("(m j) r -> m j r", j=PACK)
         for lo in (0, MID):
-            nc.scalar.copy(y01[:, 0, lo : lo + MID], multiply(out_ps, "acc", s0, lo, lo + MID)[:])
-        nc.sync.dma_start(out=out_rows[:, 0, :], in_=y01[:, 0, :])
-        acc1 = multiply(out_ps, "acc", s1, 0, R)
-        for lo in (0, MID):
-            nc.scalar.copy(y01[:, 1, lo : lo + MID], acc1[:, lo : lo + MID])
-        nc.sync.dma_start(out=out_rows[:, 1, :], in_=y01[:, 1, :])
+            for j, s_q in enumerate((s0, s1)):
+                nc.scalar.copy(y01[:, j, lo : lo + MID], multiply(out_ps, "acc", s_q, lo, lo + MID)[:])
+                if lo == MID:
+                    nc.sync.dma_start(out=out_rows[:, j, :], in_=y01[:, j, :])
         nc.scalar.copy(y23[:, 0, :], multiply(out_ps, "acc", s2, 0, R)[:])
         nc.sync.dma_start(out=out_rows[:, 2, :], in_=y23[:, 0, :])
         for lo in (0, MID):

@@ -206,18 +206,6 @@ def tile_attend_glin_q_pl_kernel(tc, kT, vT, cd, ce, doT, offs, out_0, out_1, ou
         k1_q = quantize(group(nc.scalar.copy, "k1", k1_turned), "k1")
         state1 = first_product(*k1_q)
 
-        warm = out_ps.tile([P, PACK - 1, P], F32, name="acc")
-        for t in range(PACK - 1):
-            nc.tensor.matmul_mx(
-                out=warm[:, t, :],
-                lhsT=v_q[t][0][:].bitcast(E4M3),
-                lhsT_scale=v_q[t][1][:],
-                rhs=k1_q[0][:].bitcast(E4M3),
-                rhs_scale=k1_q[1][:],
-                start=True,
-                stop=True,
-            )
-
         k2_turned = gather_and_turn(k_pool[2], "k2", K2_SHARE)
         s0_grouped = weigh(0, state0, k_bytes(2))
         s0 = quantize(s0_grouped, "s0")

@@ -245,8 +245,7 @@ def tile_attend_glin_q_pl_kernel(tc, kT, vT, cd, ce, doT, offs, out_0, out_1, ou
         for lo in (0, MID):
             for j, s_q in enumerate((s0, s1)):
                 nc.scalar.copy(y01[:, j, lo : lo + MID], multiply(out_ps, "acc", s_q, lo, lo + MID)[:])
-                if lo == MID:
-                    nc.sync.dma_start(out=out_rows[:, j, :], in_=y01[:, j, :])
+                nc.sync.dma_start(out=out_rows[:, j, lo : lo + MID], in_=y01[:, j, lo : lo + MID])
         nc.scalar.copy(y23[:, 0, :], multiply(out_ps, "acc", s2, 0, R)[:])
         nc.sync.dma_start(out=out_rows[:, 2, :], in_=y23[:, 0, :])
         for lo in (0, MID):

from contextlib import ExitStack

import concourse.mybir as mybir
from concourse.masks import make_identity

F32 = mybir.dt.float32
BF16 = mybir.dt.bfloat16
I32 = mybir.dt.int32
U32 = mybir.dt.uint32
U16 = mybir.dt.uint16
U8 = mybir.dt.uint8
E4M3 = mybir.dt.float8_e4m3fn_x4
E5M2 = mybir.dt.float8_e5m2_x4
MULT = mybir.AluOpType.mult
COPY = mybir.ActivationFunctionType.Copy

P = 128
PACK = 4
D = 512
T = 2048
SLOTS = 512
R = 512
HALF = P // 2
MID = R // 2
SHARE = 288
K2_SHARE = 192
LAST_SHARE = 256
DO_SPLIT = 192

FLOPS = 2 * D * D * SLOTS + 2 * D * D * R
BYTES = 4 * (2 * D * T + D + D + D * R + D * R) + 2 * P * SLOTS // 16 + D * R + D * R // 32


def tile_attend_glin_q_pl_kernel(tc, kT, vT, cd, ce, doT, offs, out_0, out_1, out_2):
    nc = tc.nc
    with ExitStack() as ctx:
        keep = ctx.enter_context(tc.tile_pool(name="keep", bufs=1))
        reused = ctx.enter_context(tc.tile_pool(name="reused", bufs=1))
        turn_ps = ctx.enter_context(tc.psum_pool(name="turn_ps", bufs=2))
        state_ps = ctx.enter_context(tc.psum_pool(name="state_ps", bufs=2))
        out_ps = ctx.enter_context(tc.psum_pool(name="out_ps", bufs=4))

        def sb(shape, dtype, name, offset=None):
            if offset is None:
                return keep.tile(shape, dtype, name=name, align_bytes=64)
            return reused.tile(shape, dtype, name=name, align_bytes=64, offset=offset)

        def k_bytes(j):
            return j * T * 4

        def v_bytes(t):
            return (PACK + t) * T * 4

        spare = 2 * PACK * T * 4

        offsets = keep.tile([P, SLOTS // 16], U16, name="offsets")
        v_pool = [sb([P, 2 * T], F32, "v_pool%d" % h, v_bytes(2 * h)) for h in range(2)]
        k_pool = [sb([P, T], F32, "k_pool%d" % j, k_bytes(j)) for j in range(PACK)]
        do_raw = sb([P, PACK, R], F32, "do_raw", spare)
        rows = sb([P, D], F32, "rows")
        nc.vector.memset(rows[:], 0.0)

        v_rows = vT.rearrange("(m h t) n -> m h (t n)", h=2, t=2)
        k_rows = kT.rearrange("(m j) n -> m j n", j=PACK)
        do_rows = doT.rearrange("(p t) r -> p t r", t=PACK)
        nc.sync.dma_start(out=v_pool[0][:], in_=v_rows[:, 0, :])
        nc.sync.dma_start(offsets[:], offs)
        nc.sync.dma_start(out=rows[0:1, :], in_=cd.rearrange("d o -> o d"))
        nc.sync.dma_start(out=rows[1:2, :], in_=ce[0:1, :])
        nc.sync.dma_start(out=v_pool[1][:], in_=v_rows[:, 1, :])
        for j in range(PACK):
            nc.sync.dma_start(out=k_pool[j][:], in_=k_rows[:, j, :])
        nc.sync.dma_start(out=do_raw[:], in_=do_rows)

        ident = sb([P, P], F32, "ident")
        make_identity(nc, ident[:])

        columns = sb([P, 2, PACK], F32, "columns")
        for first in (0, 2):
            columns_ps = turn_ps.tile([P, 2, P], F32, name="turned")
            for j in range(2):
                nc.tensor.transpose(columns_ps[:, j, :], rows[:, first + j :: PACK], ident[:])
            nc.scalar.copy(columns[:, :, first : first + 2], columns_ps[:, :, 0:2].rearrange("p j w -> p w j"))
        cd_col, ce_col = columns[:, 0, :], columns[:, 1, :]
        cd_rows = state_ps.tile([P, PACK, P], F32, name="state")
        for j in range(PACK):
            nc.tensor.transpose(cd_rows[:, j, :], cd_col[:, j : j + 1].to_broadcast([P, P]), ident[:])
        factor_bytes = [v_bytes(0), v_bytes(0) + 2048, k_bytes(0) + 2048, k_bytes(1) + 2048]
        factor = [sb([P, P, PACK], F32, "factor%d" % j, factor_bytes[j]) for j in range(PACK)]

        def make_factor(j):
            nc.vector.tensor_tensor(
                factor[j][:],
                cd_rows[:, j, :].unsqueeze(2).to_broadcast([P, P, PACK]),
                ce_col.unsqueeze(1).to_broadcast([P, P, PACK]),
                MULT,
            )

        def gather_and_turn(pool, name, cut, banks=(turn_ps, "turned")):
            picked = sb([P, SLOTS], BF16, name + "_picked")
            if cut > 0:
                nc.vector.tensor_copy(picked[:, :cut], pool[:].indirect(offsets[:, : cut // 16]))
            if cut < SLOTS:
                nc.scalar.activation(picked[:, cut:], pool[:].indirect(offsets[:, cut // 16 :]), COPY)
            pairs = picked[:].bitcast(F32)
            turned = banks[0].tile([P, 2, P], F32, name=banks[1])
            for u in range(2):
                nc.tensor.transpose(turned[:, u, :], pairs[:, u::2], ident[:])
            return turned

        def gather_dealt_and_turn(window, name, banks=(turn_ps, "turned")):
            picked = sb([P, SLOTS], BF16, name + "_picked")
            nc.vector.tensor_copy(picked[:].rearrange("p (u m w) -> p m u w", u=2, w=2), window.indirect(offsets[:]))
            pairs = picked[:].bitcast(F32)
            turned = banks[0].tile([P, 2, P], F32, name=banks[1])
            for u in range(2):
                nc.tensor.transpose(turned[:, u, :], pairs[:, u * P : (u + 1) * P], ident[:])
            return turned

        def group(engine_copy, name, turned, offset=None):
            grouped = sb([P, P * PACK], BF16, name + "_grouped", offset)
            engine_copy(
                grouped[:].bitcast(F32).rearrange("p (m u) -> p m u", u=2),
                turned[:].rearrange("p u m -> p m u"),
            )
            return grouped

        def quantize_columns(codes, scales, grouped, fmt, lo, hi, base=0):
            nc.vector.quantize_mx(
                out=codes[:, lo:hi].bitcast(fmt),
                scales=scales[:, lo:hi],
                in_=grouped[:, (lo - base) * PACK : (hi - base) * PACK],
            )

        def quantize(grouped, name, offset=None):
            codes = sb([P, P], U32, name + "_codes", offset)
            scales = sb([P, P], U8, name + "_scales")
            quantize_columns(codes, scales, grouped, E4M3, 0, P)
            return codes, scales

        def first_product(k_codes, k_scales):
            state = state_ps.tile([P, PACK, P], F32, name="state")
            for t in range(PACK):
                nc.tensor.matmul_mx(
                    out=state[:, t, :],
                    lhsT=v_q[t][0][:].bitcast(E4M3),
                    lhsT_scale=v_q[t][1][:],
                    rhs=k_codes[:].bitcast(E4M3),
                    rhs_scale=k_scales[:],
                    start=True,
                    stop=True,
                )
            return state

        def weigh_columns(s_grouped, j, state, lo, hi):
            nc.vector.tensor_tensor(
                s_grouped[:, lo * PACK : hi * PACK].rearrange("p (m t) -> p m t", t=PACK),
                state[:, :, lo:hi].rearrange("p t m -> p m t"),
                factor[j][:, lo:hi, :],
                MULT,
            )

        def weigh(j, state, offset=None):
            s_grouped = sb([P, P * PACK], BF16, "s%d_grouped" % j, offset)
            weigh_columns(s_grouped, j, state, 0, P)
            return s_grouped

        def places(engine_copy, grouped, planes, first, lo, hi, base=0):
            count = planes.shape[1]
            engine_copy(
                grouped[:, (lo - base) * PACK : (hi - base) * PACK].rearrange("p (c i t) -> p c t i", i=4, t=PACK)[
                    :, :, first : first + count, :
                ],
                planes[:, :, lo:hi].rearrange("p t (c i) -> p c t i", i=4),
            )

        def multiply(pool, name, s_q, lo, hi):
            acc = pool.tile([P, hi - lo], F32, name=name)
            nc.tensor.matmul_mx(
                out=acc[:],
                lhsT=s_q[0][:].bitcast(E4M3),
                lhsT_scale=s_q[1][:],
                rhs=do_codes[:, lo:hi].bitcast(E5M2),
                rhs_scale=do_scales[:, lo:hi],
                start=True,
                stop=True,
            )
            return acc

        v1 = group(nc.scalar.copy, "v1", gather_dealt_and_turn(v_pool[0][:, T:], "v1"))
        v0 = group(nc.scalar.copy, "v0", gather_and_turn(v_pool[0], "v0", SLOTS))
        v_q = [quantize(v0, "v0"), quantize(v1, "v1")]
        v3_turned = gather_dealt_and_turn(v_pool[1][:, T:], "v3", (out_ps, "acc"))
        v2_turned = gather_and_turn(v_pool[1], "v2", 0, (out_ps, "acc"))
        k0_turned = gather_and_turn(k_pool[0], "k0", SHARE)
        v3 = group(nc.scalar.copy, "v3", v3_turned, k_bytes(0))
        v2 = group(nc.scalar.copy, "v2", v2_turned, k_bytes(0) + 1024)
        for j in range(PACK - 1):
            make_factor(j)
        v3_q = quantize(v3, "v3")
        v_q.extend([quantize(v2, "v2"), v3_q])
        k1_turned = gather_and_turn(k_pool[1], "k1", SHARE)
        k0 = group(nc.scalar.copy, "k0", k0_turned, k_bytes(1))
        make_factor(3)
        state0 = first_product(*quantize(k0, "k0"))
        k1_q = quantize(group(nc.scalar.copy, "k1", k1_turned), "k1")
        state1 = first_product(*k1_q)

        k2_turned = gather_and_turn(k_pool[2], "k2", K2_SHARE)
        s0_grouped = weigh(0, state0, k_bytes(2))
        s0 = quantize(s0_grouped, "s0")
        k3_turned = gather_and_turn(k_pool[3], "k3", LAST_SHARE)
        k2 = group(nc.scalar.copy, "k2", k2_turned, k_bytes(3))
        s1_grouped = weigh(1, state1, k_bytes(3) + 1024)
        state2 = first_product(*quantize(k2, "k2"))
        s1 = quantize(s1_grouped, "s1")
        k3_q = quantize(group(nc.scalar.copy, "k3", k3_turned), "k3")
        state3 = first_product(*k3_q)

        do_codes = sb([P, R], U32, "do_codes")
        do_scales = sb([P, R], U8, "do_scales")
        do_a = sb([P, P * PACK], BF16, "do_a", k_bytes(0) + 4096)
        do_b = sb([P, P * PACK], BF16, "do_b")
        do_c = sb([P, MID * PACK], BF16, "do_c")
        places(nc.vector.tensor_copy, do_a, do_raw[:], 0, 0, P)
        places(nc.vector.tensor_copy, do_b, do_raw[:], 0, P, DO_SPLIT, P)
        places(nc.scalar.copy, do_b, do_raw[:], 0, DO_SPLIT, MID, P)
        places(nc.scalar.copy, do_c, do_raw[:], 0, MID, R, MID)
        quantize_columns(do_codes, do_scales, do_a, E5M2, 0, P)
        quantize_columns(do_codes, do_scales, do_b, E5M2, P, MID, P)
        s2_grouped = weigh(2, state2, k_bytes(0) + 4096)
        quantize_columns(do_codes, do_scales, do_c, E5M2, MID, R, MID)
        s2 = quantize(s2_grouped, "s2")
        s3_grouped = sb([P, P * PACK], BF16, "s3_grouped", spare)
        s3 = sb([P, P], U32, "s3_codes"), sb([P, P], U8, "s3_scales")
        for lo in (0, HALF):
            weigh_columns(s3_grouped, 3, state3, lo, lo + HALF)
        for lo in (0, HALF):
            quantize_columns(s3[0], s3[1], s3_grouped, E4M3, lo, lo + HALF)

        y01 = sb([P, 2, R], F32, "y01")
        y23 = sb([P, 2, R], F32, "y23")
        y_grouped = sb([P, R * PACK], BF16, "y_grouped", spare)
        out_rows = out_0.rearrange("(m j) r -> m j r", j=PACK)
        for lo in (0, MID):
            for j, s_q in enumerate((s0, s1)):
                nc.scalar.copy(y01[:, j, lo : lo + MID], multiply(out_ps, "acc", s_q, lo, lo + MID)[:])
                nc.sync.dma_start(out=out_rows[:, j, lo : lo + MID], in_=y01[:, j, lo : lo + MID])
        nc.scalar.copy(y23[:, 0, :], multiply(out_ps, "acc", s2, 0, R)[:])
        nc.sync.dma_start(out=out_rows[:, 2, :], in_=y23[:, 0, :])
        for lo in (0, MID):
            places(nc.vector.tensor_copy, y_grouped, y01[:], 0, lo, lo + MID)
        for lo in (0, MID):
            nc.scalar.copy(y23[:, 1, lo : lo + MID], multiply(turn_ps, "turned", s3, lo, lo + MID)[:])
        places(nc.vector.tensor_copy, y_grouped, y23[:], 2, 0, MID)
        places(nc.vector.tensor_copy, y_grouped, y23[:], 2, MID, 384)
        places(nc.scalar.copy, y_grouped, y23[:], 2, 384, R)
        nc.sync.dma_start(out=out_rows[:, 3, :], in_=y23[:, 1, :])
        y_codes = sb([P, R], U32, "y_codes")
        y_scales = sb([P, R], U8, "y_scales")
        words = out_1[0].rearrange("p c l -> p (c l)").bitcast(I32)
        for lo in (0, MID):
            quantize_columns(y_codes, y_scales, y_grouped, E4M3, lo, lo + MID)
            nc.sync.dma_start(out=words[:, lo : lo + MID], in_=y_codes[:, lo : lo + MID].bitcast(I32))
        for q in range(4):
            queue = nc.sync if q == 3 else nc.scalar
            queue.dma_start(
                out=out_2[0, 4 * q : 4 * q + 4, :].bitcast(I32),
                in_=y_scales[32 * q : 32 * q + 4, :].bitcast(I32),
            )
